import numpy as np
import ml_dtypes


def mxq(x, axis, fmt="e4m3"):
    dtype, down = {"e4m3": (ml_dtypes.float8_e4m3fn, 7), "e5m2": (ml_dtypes.float8_e5m2, 14)}[fmt]
    v = np.moveaxis(np.asarray(x, np.float32).astype(ml_dtypes.bfloat16).astype(np.float64), axis, -1)
    blocks = v.reshape(v.shape[:-1] + (-1, 32))
    amax = np.abs(blocks).max(-1, keepdims=True)
    byte = np.maximum(np.where(amax > 0, np.frexp(amax)[1] - 1 + 127, 0) - down, 1)
    scale = np.exp2(byte - 127.0)
    codes = (blocks / scale).astype(np.float32).astype(dtype).astype(np.float64)
    return np.moveaxis((codes * scale).reshape(v.shape), -1, axis)


WIDE = False


def mx_kscale(k):
    if not WIDE:
        return np.ones(k)
    levels = np.array([10, -10, 5, -5, 0])
    if k % 512:
        return np.exp2(np.random.permutation(np.resize(levels, k // 32))).repeat(32)
    a = np.empty((k // 512, 16))
    for p in range(k // 512):
        a[p, :8] = np.random.permutation(np.resize(levels, 8))
        for g in range(8):
            far = levels[np.abs(levels - a[p, g]) >= 10]
            a[p, g + 8] = far[np.random.randint(len(far))]
    return np.exp2(a.ravel()).repeat(32)


def f64(x):
    return np.asarray(x).astype(np.float64)


def striped(idx):
    return np.tile(idx.reshape(-1, 16).T, (8, 1)).astype(np.uint16)


def unstriped(offs):
    return offs[:16].T.reshape(-1).astype(np.int64)


def pack_weight(w):
    k, n = w.shape
    w = f64(np.asarray(w, np.float32).astype(ml_dtypes.bfloat16)).reshape(k // 32, 32, n)
    amax = np.abs(w).max(1)
    byte = np.clip(np.where(amax > 0, np.frexp(amax)[1] - 1 + 127 - 7, 1), 1, 254)
    scaled = (w * np.exp2(127.0 - byte)[:, None, :]).reshape(k, n).astype(np.float32)
    words = np.ascontiguousarray(scaled.reshape(k // 512, 128, 4, n).transpose(0, 1, 3, 2)).astype(ml_dtypes.float8_e4m3fn).view(np.uint8)
    return words, np.ascontiguousarray(byte.astype(np.uint8).reshape(k // 512, 16, n))


def unpack_weight(words, scales):
    g, p, n, _ = words.shape
    vals = np.ascontiguousarray(words).view(ml_dtypes.float8_e4m3fn).astype(np.float64) * np.repeat(np.exp2(scales.astype(np.float64) - 127.0), 8, axis=1)[..., None]
    return vals.transpose(0, 1, 3, 2).reshape(g * 512, n)


K, T, S, D, G, J = 1024, 4096, 1024, 4, 256, 512


def setup_inputs():
    n = np.random.standard_normal
    s = mx_kscale(K)[:, None]
    packed_xT = pack_weight(n((K, T)) * s)
    return {
        "x_words": packed_xT[0],
        "x_scales": packed_xT[1],
        "hT": (n((K, J)) / np.sqrt(K) / s).astype(np.float32),
        "offs": striped(np.random.permutation(T)[:S]),
    }


def reference(x_words, x_scales, hT, offs):
    hTq = mxq(f64(hT), 0, "e4m3")
    xq = unpack_weight(x_words, x_scales)[:, unstriped(offs)]
    y = hTq.T @ xq
    return y.reshape(J, G, D).max(axis=2)

@@ -1,0 +1,172 @@
+from contextlib import ExitStack
+
+import concourse.mybir as mybir
+
+K, T, S, D, J = 1024, 4096, 1024, 4, 512
+FLOPS = 2 * K * J * S
+
+F32 = mybir.dt.float32
+BF16 = mybir.dt.bfloat16
+I32 = mybir.dt.int32
+U32 = mybir.dt.uint32
+U16 = mybir.dt.uint16
+U8 = mybir.dt.uint8
+FP8X4 = mybir.dt.float8_e4m3fn_x4
+MAX = mybir.AluOpType.max
+
+P = 128
+PACK = 4
+K_PASS = P * PACK
+PASSES = K // K_PASS
+N = 512
+HALVES = S // N
+Q_TILES = J // P
+LIST_COLS = N // 16
+DOCS = N // D
+
+
+def tile_picked_zlate_max_p_kernel(tc, x_words, x_scales, hT, offs, out):
+    nc = tc.nc
+    with ExitStack() as ctx:
+        keep = ctx.enter_context(tc.tile_pool(name="keep", bufs=1))
+        psum = ctx.enter_context(tc.psum_pool(name="psum", bufs=1))
+
+        scale_table = keep.tile([P, T], U8, name="scale_table", align_bytes=64)
+        nc.vector.memset(scale_table[:].bitcast(I32), 0)
+
+        word_table = [keep.tile([P, T], I32, name="word_table%d" % o, align_bytes=64) for o in range(PASSES)]
+        offsets = keep.tile([P, S // 16], U16, name="offsets")
+
+        def load_words(o):
+            nc.sync.dma_start(out=word_table[o][:], in_=x_words[o].rearrange("p n t -> p (n t)").bitcast(I32))
+
+        load_words(0)
+        nc.sync.dma_start(offsets[:], offs)
+        for q in range(4):
+            nc.sync.dma_start(
+                out=scale_table[32 * q : 32 * q + 8, :].bitcast(I32),
+                in_=x_scales[:, 4 * q : 4 * q + 4, :].bitcast(I32),
+            )
+        load_words(1)
+
+        h_raw = {}
+        for t in range(Q_TILES):
+            for o in range(PASSES):
+                h_raw[t, o] = keep.tile([P, PACK, P], F32, name="h_raw%d_%d" % (t, o), align_bytes=64)
+                rows = hT[o * K_PASS : (o + 1) * K_PASS, t * P : (t + 1) * P]
+                nc.sync.dma_start(out=h_raw[t, o][:], in_=rows.rearrange("(p j) c -> p j c", j=PACK))
+
+        x_scale = keep.tile([P, S], U8, name="x_scale", align_bytes=64)
+        x_code = {}
+
+        def gather_words(o, h, tag):
+            x_code[o, h] = keep.tile([P, N], U32, name="x_code%d_%d" % (o, h), tag=tag, align_bytes=64)
+            part = offsets[:, h * LIST_COLS : (h + 1) * LIST_COLS]
+            nc.vector.tensor_copy(x_code[o, h][:], word_table[o][:].bitcast(U32).indirect(part))
+
+        first_bf = keep.tile([P, 1, P, PACK], BF16, name="first_bf", align_bytes=64)
+        h_bf = [keep.tile([P, PASSES, P, PACK], BF16, name="h_bf%d" % t, align_bytes=64) for t in range(Q_TILES)]
+        h_code = [keep.tile([P, PASSES, P], U32, name="h_code%d" % t, align_bytes=64) for t in range(Q_TILES)]
+        h_scale = [keep.tile([P, PASSES, P], U8, name="h_scale%d" % t, align_bytes=64) for t in range(Q_TILES)]
+        bank = {}
+        for t in range(Q_TILES):
+            for h in range(HALVES):
+                bank[t, h] = psum.tile([P, N], F32, name="bank%d_%d" % (t, h))
+
+        def rounded(t, o):
+            return first_bf[:, 0] if (t, o) == (0, 0) else h_bf[t][:, o]
+
+        def interleave(t, o):
+            nc.scalar.copy(
+                out=rounded(t, o).rearrange("p (c i) j -> p c j i", i=4),
+                in_=h_raw[t, o][:].rearrange("p j (c i) -> p c j i", i=4),
+            )
+
+        def quantize_pass(t, o):
+            nc.vector.quantize_mx(
+                out=h_code[t][:, o, :].bitcast(FP8X4),
+                scales=h_scale[t][:, o, :],
+                in_=rounded(t, o).rearrange("p c j -> p (c j)"),
+            )
+
+        def quantize_tile(t):
+            nc.vector.quantize_mx(
+                out=h_code[t][:].rearrange("p o c -> p (o c)").bitcast(FP8X4),
+                scales=h_scale[t][:].rearrange("p o c -> p (o c)"),
+                in_=h_bf[t][:].rearrange("p o c j -> p (o c j)"),
+            )
+
+        def multiply(t, o, h):
+            nc.tensor.matmul_mx(
+                out=bank[t, h][:],
+                lhsT=h_code[t][:, o, :].bitcast(FP8X4),
+                lhsT_scale=h_scale[t][:, o, :],
+                rhs=x_code[o, h][:].bitcast(FP8X4),
+                rhs_scale=x_scale[4 * o : P, h * N : (h + 1) * N],
+                start=(o == 0),
+                stop=(o == PASSES - 1),
+            )
+
+        def store(t, cols, best):
+            nc.sync.dma_start(out=out[t * P : (t + 1) * P, cols], in_=best)
+
+        def pool_max(t, h, tag):
+            best = keep.tile([P, DOCS], F32, name="best%d_%d" % (t, h), tag=tag, align_bytes=64)
+            nc.vector.tensor_reduce(
+                out=best[:],
+                in_=bank[t, h][:].rearrange("p (v d) -> p v d", d=D),
+                axis=mybir.AxisListType.X,
+                op=MAX,
+            )
+            store(t, slice(h * DOCS, (h + 1) * DOCS), best[:])
+
+        pair = {}
+
+        def first_max(t, h):
+            if h == 0:
+                tag = "h_bf3" if t == 1 else "pair%d" % t
+                pair[t] = keep.tile([P, HALVES, 2, DOCS], F32, name="pair%d" % t, tag=tag, align_bytes=64)
+            by_token = bank[t, h][:].rearrange("p (v d) -> p d v", d=D)
+            side = keep.tile([P, 2, DOCS], F32, name="side%d_%d" % (t, h))
+            nc.scalar.copy(out=side[:], in_=by_token[:, 2:4, :])
+            nc.vector.tensor_tensor(out=pair[t][:, h], in0=by_token[:, 0:2, :], in1=side[:], op=MAX)
+
+        def second_max(t, parts):
+            best = keep.tile([P, HALVES, DOCS], F32, name="best%d" % t, align_bytes=64)
+            for hs in parts:
+                nc.vector.tensor_tensor(out=best[:, hs], in0=pair[t][:, hs, 0, :], in1=pair[t][:, hs, 1, :], op=MAX)
+            store(t, slice(0, HALVES * DOCS), best[:].rearrange("p h v -> p (h v)"))
+
+        def multiply_tile(t):
+            for h in range(HALVES):
+                for o in range(PASSES):
+                    multiply(t, o, h)
+
+        for h in range(HALVES):
+            gather_words(0, h, "x_code0_%d" % h)
+        nc.vector.tensor_copy(x_scale[:], scale_table[:].indirect(offsets[:]))
+        for t in range(Q_TILES):
+            for o in range(PASSES):
+                interleave(t, o)
+        gather_words(1, 0, "x_code1_0")
+        quantize_pass(0, 0)
+        gather_words(1, 1, "first_bf")
+        quantize_pass(0, 1)
+        for o in range(PASSES):
+            for h in range(HALVES):
+                multiply(0, o, h)
+        for h in range(HALVES):
+            quantize_tile(1 + h)
+            multiply_tile(1 + h)
+            pool_max(0, h, "h_bf%d" % (1 + h))
+        quantize_tile(3)
+        multiply_tile(3)
+        first_max(1, 0)
+        first_max(1, 1)
+        first_max(2, 0)
+        second_max(1, [slice(0, 2)])
+        first_max(2, 1)
+        first_max(3, 0)
+        second_max(2, [slice(0, 2)])
+        first_max(3, 1)
+        second_max(3, [slice(0, 1), slice(1, 2)])

@@ -43,18 +43,20 @@ def tile_picked_zlate_max_p_kernel(tc, x_words, x_scales, hT, offs, out):
         load_words(0)
         nc.sync.dma_start(offsets[:], offs)
         for q in range(4):
-            nc.sync.dma_start(
+            nc.gpsimd.dma_start(
                 out=scale_table[32 * q : 32 * q + 8, :].bitcast(I32),
                 in_=x_scales[:, 4 * q : 4 * q + 4, :].bitcast(I32),
             )
         load_words(1)
 
+        pieces = [(t, 1, o) for t in range(Q_TILES) for o in range(PASSES)]
         h_raw = {}
-        for t in range(Q_TILES):
-            for o in range(PASSES):
-                h_raw[t, o] = keep.tile([P, PACK, P], F32, name="h_raw%d_%d" % (t, o), align_bytes=64)
-                rows = hT[o * K_PASS : (o + 1) * K_PASS, t * P : (t + 1) * P]
-                nc.sync.dma_start(out=h_raw[t, o][:], in_=rows.rearrange("(p j) c -> p j c", j=PACK))
+        for t0, tiles, o in pieces:
+            raw = keep.tile([P, PACK, tiles * P], F32, name="h_raw%d_%d" % (t0, o), align_bytes=64)
+            rows = hT[o * K_PASS : (o + 1) * K_PASS, t0 * P : (t0 + tiles) * P]
+            nc.sync.dma_start(out=raw[:], in_=rows.rearrange("(p j) c -> p j c", j=PACK))
+            for i in range(tiles):
+                h_raw[t0 + i, o] = raw[:, :, i * P : (i + 1) * P]
 
         x_scale = keep.tile([P, S], U8, name="x_scale", align_bytes=64)
         x_code = {}
@@ -64,43 +66,41 @@ def tile_picked_zlate_max_p_kernel(tc, x_words, x_scales, hT, offs, out):
             part = offsets[:, h * LIST_COLS : (h + 1) * LIST_COLS]
             nc.vector.tensor_copy(x_code[o, h][:], word_table[o][:].bitcast(U32).indirect(part))
 
-        first_bf = keep.tile([P, 1, P, PACK], BF16, name="first_bf", align_bytes=64)
-        h_bf = [keep.tile([P, PASSES, P, PACK], BF16, name="h_bf%d" % t, align_bytes=64) for t in range(Q_TILES)]
-        h_code = [keep.tile([P, PASSES, P], U32, name="h_code%d" % t, align_bytes=64) for t in range(Q_TILES)]
-        h_scale = [keep.tile([P, PASSES, P], U8, name="h_scale%d" % t, align_bytes=64) for t in range(Q_TILES)]
+        groups = [(t, 1, o) for t in range(Q_TILES) for o in range(PASSES)]
+        h_bf, h_code, h_scale, whole = {}, {}, {}, {}
+        for t0, tiles, o in groups:
+            bf = keep.tile([P, tiles, P, PACK], BF16, name="h_bf%d_%d" % (t0, o), align_bytes=64)
+            code = keep.tile([P, tiles * P], U32, name="h_code%d_%d" % (t0, o), align_bytes=64)
+            scale = keep.tile([P, tiles * P], U8, name="h_scale%d_%d" % (t0, o), align_bytes=64)
+            whole[t0, o] = (bf, code, scale)
+            for i in range(tiles):
+                h_bf[t0 + i, o] = bf[:, i]
+                h_code[t0 + i, o] = code[:, i * P : (i + 1) * P]
+                h_scale[t0 + i, o] = scale[:, i * P : (i + 1) * P]
         bank = {}
         for t in range(Q_TILES):
             for h in range(HALVES):
                 bank[t, h] = psum.tile([P, N], F32, name="bank%d_%d" % (t, h))
 
-        def rounded(t, o):
-            return first_bf[:, 0] if (t, o) == (0, 0) else h_bf[t][:, o]
-
         def interleave(t, o):
             nc.scalar.copy(
-                out=rounded(t, o).rearrange("p (c i) j -> p c j i", i=4),
-                in_=h_raw[t, o][:].rearrange("p j (c i) -> p c j i", i=4),
+                out=h_bf[t, o].rearrange("p (c i) j -> p c j i", i=4),
+                in_=h_raw[t, o].rearrange("p j (c i) -> p c j i", i=4),
             )
 
-        def quantize_pass(t, o):
+        def quantize(t0, o):
+            bf, code, scale = whole[t0, o]
             nc.vector.quantize_mx(
-                out=h_code[t][:, o, :].bitcast(FP8X4),
-                scales=h_scale[t][:, o, :],
-                in_=rounded(t, o).rearrange("p c j -> p (c j)"),
-            )
-
-        def quantize_tile(t):
-            nc.vector.quantize_mx(
-                out=h_code[t][:].rearrange("p o c -> p (o c)").bitcast(FP8X4),
-                scales=h_scale[t][:].rearrange("p o c -> p (o c)"),
-                in_=h_bf[t][:].rearrange("p o c j -> p (o c j)"),
+                out=code[:].bitcast(FP8X4),
+                scales=scale[:],
+                in_=bf[:].rearrange("p i c j -> p (i c j)"),
             )
 
         def multiply(t, o, h):
             nc.tensor.matmul_mx(
                 out=bank[t, h][:],
-                lhsT=h_code[t][:, o, :].bitcast(FP8X4),
-                lhsT_scale=h_scale[t][:, o, :],
+                lhsT=h_code[t, o].bitcast(FP8X4),
+                lhsT_scale=h_scale[t, o],
                 rhs=x_code[o, h][:].bitcast(FP8X4),
                 rhs_scale=x_scale[4 * o : P, h * N : (h + 1) * N],
                 start=(o == 0),
@@ -120,53 +120,23 @@ def tile_picked_zlate_max_p_kernel(tc, x_words, x_scales, hT, offs, out):
             )
             store(t, slice(h * DOCS, (h + 1) * DOCS), best[:])
 
-        pair = {}
-
-        def first_max(t, h):
-            if h == 0:
-                tag = "h_bf3" if t == 1 else "pair%d" % t
-                pair[t] = keep.tile([P, HALVES, 2, DOCS], F32, name="pair%d" % t, tag=tag, align_bytes=64)
-            by_token = bank[t, h][:].rearrange("p (v d) -> p d v", d=D)
-            side = keep.tile([P, 2, DOCS], F32, name="side%d_%d" % (t, h))
-            nc.scalar.copy(out=side[:], in_=by_token[:, 2:4, :])
-            nc.vector.tensor_tensor(out=pair[t][:, h], in0=by_token[:, 0:2, :], in1=side[:], op=MAX)
-
-        def second_max(t, parts):
-            best = keep.tile([P, HALVES, DOCS], F32, name="best%d" % t, align_bytes=64)
-            for hs in parts:
-                nc.vector.tensor_tensor(out=best[:, hs], in0=pair[t][:, hs, 0, :], in1=pair[t][:, hs, 1, :], op=MAX)
-            store(t, slice(0, HALVES * DOCS), best[:].rearrange("p h v -> p (h v)"))
-
-        def multiply_tile(t):
-            for h in range(HALVES):
-                for o in range(PASSES):
-                    multiply(t, o, h)
-
         for h in range(HALVES):
             gather_words(0, h, "x_code0_%d" % h)
         nc.vector.tensor_copy(x_scale[:], scale_table[:].indirect(offsets[:]))
         for t in range(Q_TILES):
             for o in range(PASSES):
                 interleave(t, o)
-        gather_words(1, 0, "x_code1_0")
-        quantize_pass(0, 0)
-        gather_words(1, 1, "first_bf")
-        quantize_pass(0, 1)
+        gather_words(1, 0, "scale_table")
+        quantize(0, 0)
+        gather_words(1, 1, "h_bf0_0")
+        quantize(0, 1)
         for o in range(PASSES):
             for h in range(HALVES):
                 multiply(0, o, h)
-        for h in range(HALVES):
-            quantize_tile(1 + h)
-            multiply_tile(1 + h)
-            pool_max(0, h, "h_bf%d" % (1 + h))
-        quantize_tile(3)
-        multiply_tile(3)
-        first_max(1, 0)
-        first_max(1, 1)
-        first_max(2, 0)
-        second_max(1, [slice(0, 2)])
-        first_max(2, 1)
-        first_max(3, 0)
-        second_max(2, [slice(0, 2)])
-        first_max(3, 1)
-        second_max(3, [slice(0, 1), slice(1, 2)])
+        for t in range(Q_TILES):
+            for h in range(HALVES):
+                if t + 1 < Q_TILES:
+                    quantize(t + 1, h)
+                    for g in range(HALVES):
+                        multiply(t + 1, h, g)
+                pool_max(t, h, "h_bf%d_%d" % (t + 1, h))

@@ -23,6 +23,7 @@ HALVES = S // N
 Q_TILES = J // P
 LIST_COLS = N // 16
 DOCS = N // D
+HEAD = 1024
 
 
 def tile_picked_zlate_max_p_kernel(tc, x_words, x_scales, hT, offs, out):
@@ -37,17 +38,30 @@ def tile_picked_zlate_max_p_kernel(tc, x_words, x_scales, hT, offs, out):
         word_table = [keep.tile([P, T], I32, name="word_table%d" % o, align_bytes=64) for o in range(PASSES)]
         offsets = keep.tile([P, S // 16], U16, name="offsets")
 
-        def load_words(o):
-            nc.sync.dma_start(out=word_table[o][:], in_=x_words[o].rearrange("p n t -> p (n t)").bitcast(I32))
+        def load_words(o, cols):
+            words = x_words[o].rearrange("p n t -> p (n t)").bitcast(I32)
+            nc.sync.dma_start(out=word_table[o][:, cols], in_=words[:, cols])
 
-        load_words(0)
+        load_words(0, slice(0, HEAD))
         nc.sync.dma_start(offsets[:], offs)
-        for q in range(4):
-            nc.gpsimd.dma_start(
-                out=scale_table[32 * q : 32 * q + 8, :].bitcast(I32),
-                in_=x_scales[:, 4 * q : 4 * q + 4, :].bitcast(I32),
-            )
-        load_words(1)
+        nc.sync.dma_start(
+            out=scale_table[0:P:4, :].bitcast(I32),
+            in_=x_scales.rearrange("o m c -> m o c").bitcast(I32),
+        )
+        load_words(0, slice(HEAD, T))
+        load_words(1, slice(0, T // 2))
+
+        picked = keep.tile([P, S], U8, name="picked", align_bytes=64)
+        x_scale = keep.tile([P, S], U8, name="x_scale", align_bytes=64)
+        nc.vector.tensor_copy(picked[:], scale_table[:].indirect(offsets[:]))
+        nc.vector.tensor_copy(x_scale[:].bitcast(I32), picked[:].bitcast(I32))
+        for o in range(PASSES):
+            for i in range(1, 4):
+                nc.sync.dma_start(
+                    out=x_scale[4 * o + i : P : 32, :].bitcast(I32),
+                    in_=picked[4 * o + 8 * i : P : 32, :].bitcast(I32),
+                )
+        load_words(1, slice(T // 2, T))
 
         pieces = [(t, 1, o) for t in range(Q_TILES) for o in range(PASSES)]
         h_raw = {}
@@ -58,7 +72,6 @@ def tile_picked_zlate_max_p_kernel(tc, x_words, x_scales, hT, offs, out):
             for i in range(tiles):
                 h_raw[t0 + i, o] = raw[:, :, i * P : (i + 1) * P]
 
-        x_scale = keep.tile([P, S], U8, name="x_scale", align_bytes=64)
         x_code = {}
 
         def gather_words(o, h, tag):
@@ -122,11 +135,10 @@ def tile_picked_zlate_max_p_kernel(tc, x_words, x_scales, hT, offs, out):
 
         for h in range(HALVES):
             gather_words(0, h, "x_code0_%d" % h)
-        nc.vector.tensor_copy(x_scale[:], scale_table[:].indirect(offsets[:]))
         for t in range(Q_TILES):
             for o in range(PASSES):
                 interleave(t, o)
-        gather_words(1, 0, "scale_table")
+        gather_words(1, 0, "x_code1_0")
         quantize(0, 0)
         gather_words(1, 1, "h_bf0_0")
         quantize(0, 1)

@@ -109,6 +109,17 @@ def tile_picked_zlate_max_p_kernel(tc, x_words, x_scales, hT, offs, out):
                 in_=bf[:].rearrange("p i c j -> p (i c j)"),
             )
 
+        def warm():
+            nc.tensor.matmul_mx(
+                out=bank[3, 1][:],
+                lhsT=x_code[0, 0][:, 0:P].bitcast(FP8X4),
+                lhsT_scale=x_scale[:, 0:P],
+                rhs=x_code[0, 0][:].bitcast(FP8X4),
+                rhs_scale=x_scale[:, 0:N],
+                start=True,
+                stop=True,
+            )
+
         def multiply(t, o, h):
             nc.tensor.matmul_mx(
                 out=bank[t, h][:],
@@ -138,6 +149,8 @@ def tile_picked_zlate_max_p_kernel(tc, x_words, x_scales, hT, offs, out):
         for t in range(Q_TILES):
             for o in range(PASSES):
                 interleave(t, o)
+        for repeat in range(4):
+            warm()
         gather_words(1, 0, "x_code1_0")
         quantize(0, 0)
         gather_words(1, 1, "h_bf0_0")

@@ -42,6 +42,13 @@ def tile_picked_zlate_max_p_kernel(tc, x_words, x_scales, hT, offs, out):
             words = x_words[o].rearrange("p n t -> p (n t)").bitcast(I32)
             nc.sync.dma_start(out=word_table[o][:, cols], in_=words[:, cols])
 
+        h_raw = {}
+
+        def load_queries(t, o):
+            h_raw[t, o] = keep.tile([P, PACK, P], F32, name="h_raw%d_%d" % (t, o), align_bytes=64)
+            rows = hT[o * K_PASS : (o + 1) * K_PASS, t * P : (t + 1) * P]
+            nc.sync.dma_start(out=h_raw[t, o][:], in_=rows.rearrange("(p j) c -> p j c", j=PACK))
+
         load_words(0, slice(0, HEAD))
         nc.sync.dma_start(offsets[:], offs)
         nc.sync.dma_start(
@@ -52,25 +59,22 @@ def tile_picked_zlate_max_p_kernel(tc, x_words, x_scales, hT, offs, out):
         load_words(1, slice(0, T // 2))
 
         picked = keep.tile([P, S], U8, name="picked", align_bytes=64)
-        x_scale = keep.tile([P, S], U8, name="x_scale", align_bytes=64)
+        x_scale = [keep.tile([P, S], U8, name="x_scale%d" % o, align_bytes=64) for o in range(PASSES)]
         nc.vector.tensor_copy(picked[:], scale_table[:].indirect(offsets[:]))
-        nc.vector.tensor_copy(x_scale[:].bitcast(I32), picked[:].bitcast(I32))
         for o in range(PASSES):
+            nc.vector.tensor_copy(x_scale[o][:].bitcast(I32), picked[:].bitcast(I32))
             for i in range(1, 4):
                 nc.sync.dma_start(
-                    out=x_scale[4 * o + i : P : 32, :].bitcast(I32),
+                    out=x_scale[o][4 * o + i : P : 32, :].bitcast(I32),
                     in_=picked[4 * o + 8 * i : P : 32, :].bitcast(I32),
                 )
-        load_words(1, slice(T // 2, T))
+            if o == 0:
+                load_words(1, slice(T // 2, T))
 
-        pieces = [(t, 1, o) for t in range(Q_TILES) for o in range(PASSES)]
-        h_raw = {}
-        for t0, tiles, o in pieces:
-            raw = keep.tile([P, PACK, tiles * P], F32, name="h_raw%d_%d" % (t0, o), align_bytes=64)
-            rows = hT[o * K_PASS : (o + 1) * K_PASS, t0 * P : (t0 + tiles) * P]
-            nc.sync.dma_start(out=raw[:], in_=rows.rearrange("(p j) c -> p j c", j=PACK))
-            for i in range(tiles):
-                h_raw[t0 + i, o] = raw[:, :, i * P : (i + 1) * P]
+        for t in range(Q_TILES):
+            for o in range(PASSES):
+                if (t, o) not in h_raw:
+                    load_queries(t, o)
 
         x_code = {}
 
@@ -79,45 +83,36 @@ def tile_picked_zlate_max_p_kernel(tc, x_words, x_scales, hT, offs, out):
             part = offsets[:, h * LIST_COLS : (h + 1) * LIST_COLS]
             nc.vector.tensor_copy(x_code[o, h][:], word_table[o][:].bitcast(U32).indirect(part))
 
-        groups = [(t, 1, o) for t in range(Q_TILES) for o in range(PASSES)]
         h_bf, h_code, h_scale, whole = {}, {}, {}, {}
-        for t0, tiles, o in groups:
-            bf = keep.tile([P, tiles, P, PACK], BF16, name="h_bf%d_%d" % (t0, o), align_bytes=64)
-            code = keep.tile([P, tiles * P], U32, name="h_code%d_%d" % (t0, o), align_bytes=64)
-            scale = keep.tile([P, tiles * P], U8, name="h_scale%d_%d" % (t0, o), align_bytes=64)
-            whole[t0, o] = (bf, code, scale)
-            for i in range(tiles):
-                h_bf[t0 + i, o] = bf[:, i]
-                h_code[t0 + i, o] = code[:, i * P : (i + 1) * P]
-                h_scale[t0 + i, o] = scale[:, i * P : (i + 1) * P]
+
+        def group(t, passes, code_tag=None):
+            name = "%d_%d" % (t, passes[0])
+            bf = keep.tile([P, len(passes), P, PACK], BF16, name="h_bf" + name, align_bytes=64)
+            code = keep.tile([P, len(passes) * P], U32, name="h_code" + name, tag=code_tag or "h_code" + name, align_bytes=64)
+            scale = keep.tile([P, len(passes) * P], U8, name="h_scale" + name, align_bytes=64)
+            whole[t, passes[0]] = (bf, code, scale)
+            for i, o in enumerate(passes):
+                h_bf[t, o] = bf[:, i]
+                h_code[t, o] = code[:, i * P : (i + 1) * P]
+                h_scale[t, o] = scale[:, i * P : (i + 1) * P]
+
         bank = {}
         for t in range(Q_TILES):
             for h in range(HALVES):
                 bank[t, h] = psum.tile([P, N], F32, name="bank%d_%d" % (t, h))
 
-        def interleave(t, o):
-            nc.scalar.copy(
+        def interleave(t, o, copy):
+            copy(
                 out=h_bf[t, o].rearrange("p (c i) j -> p c j i", i=4),
-                in_=h_raw[t, o].rearrange("p j (c i) -> p c j i", i=4),
+                in_=h_raw[t, o][:].rearrange("p j (c i) -> p c j i", i=4),
             )
 
-        def quantize(t0, o):
-            bf, code, scale = whole[t0, o]
+        def quantize(t, o):
+            bf, code, scale = whole[t, o]
             nc.vector.quantize_mx(
                 out=code[:].bitcast(FP8X4),
                 scales=scale[:],
                 in_=bf[:].rearrange("p i c j -> p (i c j)"),
-            )
-
-        def warm():
-            nc.tensor.matmul_mx(
-                out=bank[3, 1][:],
-                lhsT=x_code[0, 0][:, 0:P].bitcast(FP8X4),
-                lhsT_scale=x_scale[:, 0:P],
-                rhs=x_code[0, 0][:].bitcast(FP8X4),
-                rhs_scale=x_scale[:, 0:N],
-                start=True,
-                stop=True,
             )
 
         def multiply(t, o, h):
@@ -126,13 +121,10 @@ def tile_picked_zlate_max_p_kernel(tc, x_words, x_scales, hT, offs, out):
                 lhsT=h_code[t, o].bitcast(FP8X4),
                 lhsT_scale=h_scale[t, o],
                 rhs=x_code[o, h][:].bitcast(FP8X4),
-                rhs_scale=x_scale[4 * o : P, h * N : (h + 1) * N],
+                rhs_scale=x_scale[o][4 * o : P, h * N : (h + 1) * N],
                 start=(o == 0),
                 stop=(o == PASSES - 1),
             )
-
-        def store(t, cols, best):
-            nc.sync.dma_start(out=out[t * P : (t + 1) * P, cols], in_=best)
 
         def pool_max(t, h, tag):
             best = keep.tile([P, DOCS], F32, name="best%d_%d" % (t, h), tag=tag, align_bytes=64)
@@ -142,26 +134,55 @@ def tile_picked_zlate_max_p_kernel(tc, x_words, x_scales, hT, offs, out):
                 axis=mybir.AxisListType.X,
                 op=MAX,
             )
-            store(t, slice(h * DOCS, (h + 1) * DOCS), best[:])
+            nc.sync.dma_start(out=out[t * P : (t + 1) * P, h * DOCS : (h + 1) * DOCS], in_=best[:])
 
+        def tile_max(t, tag):
+            best = keep.tile([P, HALVES, DOCS], F32, name="best%d" % t, tag=tag, align_bytes=64)
+            for h in range(HALVES):
+                nc.vector.tensor_reduce(
+                    out=best[:, h],
+                    in_=bank[t, h][:].rearrange("p (v d) -> p v d", d=D),
+                    axis=mybir.AxisListType.X,
+                    op=MAX,
+                )
+            nc.sync.dma_start(out=out[t * P : (t + 1) * P, :], in_=best[:].rearrange("p h v -> p (h v)"))
+
+        group(0, [0])
+        for t in range(1, Q_TILES):
+            group(t, [0, 1])
         for h in range(HALVES):
             gather_words(0, h, "x_code0_%d" % h)
+        for repeat in range(4):
+            nc.tensor.matmul_mx(
+                out=bank[Q_TILES - 1, HALVES - 1][:],
+                lhsT=x_code[0, 0][:, 0:P].bitcast(FP8X4),
+                lhsT_scale=x_scale[0][0:P, 0:P],
+                rhs=x_code[0, 0][:].bitcast(FP8X4),
+                rhs_scale=x_scale[0][0:P, 0:N],
+                start=True,
+                stop=True,
+            )
+        group(0, [1], "h_bf0_0")
         for t in range(Q_TILES):
             for o in range(PASSES):
-                interleave(t, o)
-        for repeat in range(4):
-            warm()
+                if (t, o) != (0, 1):
+                    interleave(t, o, nc.scalar.copy)
         gather_words(1, 0, "x_code1_0")
+        interleave(0, 1, nc.vector.tensor_copy)
         quantize(0, 0)
-        gather_words(1, 1, "h_bf0_0")
         quantize(0, 1)
+        gather_words(1, 1, "h_bf0_1")
         for o in range(PASSES):
             for h in range(HALVES):
                 multiply(0, o, h)
-        for t in range(Q_TILES):
+        for t in range(1, Q_TILES):
+            quantize(t, 0)
             for h in range(HALVES):
-                if t + 1 < Q_TILES:
-                    quantize(t + 1, h)
-                    for g in range(HALVES):
-                        multiply(t + 1, h, g)
-                pool_max(t, h, "h_bf%d_%d" % (t + 1, h))
+                for o in range(PASSES):
+                    multiply(t, o, h)
+        tile_max(0, "h_bf1_0")
+        pool_max(1, 0, "h_bf2_0")
+        pool_max(1, 1, "h_bf3_0")
+        tile_max(2, "best2")
+        pool_max(3, 0, "best3_0")
+        pool_max(3, 1, "best3_1")

@@ -56,7 +56,7 @@ def tile_picked_zlate_max_p_kernel(tc, x_words, x_scales, hT, offs, out):
             in_=x_scales.rearrange("o m c -> m o c").bitcast(I32),
         )
         load_words(0, slice(HEAD, T))
-        load_words(1, slice(0, T // 2))
+        load_words(1, slice(0, T - HEAD))
 
         picked = keep.tile([P, S], U8, name="picked", align_bytes=64)
         x_scale = [keep.tile([P, S], U8, name="x_scale%d" % o, align_bytes=64) for o in range(PASSES)]
@@ -69,7 +69,9 @@ def tile_picked_zlate_max_p_kernel(tc, x_words, x_scales, hT, offs, out):
                     in_=picked[4 * o + 8 * i : P : 32, :].bitcast(I32),
                 )
             if o == 0:
-                load_words(1, slice(T // 2, T))
+                load_words(1, slice(T - HEAD, T))
+                load_queries(0, 0)
+                load_queries(0, 1)
 
         for t in range(Q_TILES):
             for o in range(PASSES):

@@ -154,16 +154,6 @@ def tile_picked_zlate_max_p_kernel(tc, x_words, x_scales, hT, offs, out):
             group(t, [0, 1])
         for h in range(HALVES):
             gather_words(0, h, "x_code0_%d" % h)
-        for repeat in range(4):
-            nc.tensor.matmul_mx(
-                out=bank[Q_TILES - 1, HALVES - 1][:],
-                lhsT=x_code[0, 0][:, 0:P].bitcast(FP8X4),
-                lhsT_scale=x_scale[0][0:P, 0:P],
-                rhs=x_code[0, 0][:].bitcast(FP8X4),
-                rhs_scale=x_scale[0][0:P, 0:N],
-                start=True,
-                stop=True,
-            )
         group(0, [1], "h_bf0_0")
         for t in range(Q_TILES):
             for o in range(PASSES):
@@ -174,8 +164,8 @@ def tile_picked_zlate_max_p_kernel(tc, x_words, x_scales, hT, offs, out):
         quantize(0, 0)
         quantize(0, 1)
         gather_words(1, 1, "h_bf0_1")
-        for o in range(PASSES):
-            for h in range(HALVES):
+        for h in range(HALVES):
+            for o in range(PASSES):
                 multiply(0, o, h)
         for t in range(1, Q_TILES):
             quantize(t, 0)

@@ -30,6 +30,7 @@ def tile_picked_zlate_max_p_kernel(tc, x_words, x_scales, hT, offs, out):
     nc = tc.nc
     with ExitStack() as ctx:
         keep = ctx.enter_context(tc.tile_pool(name="keep", bufs=1))
+        shared = ctx.enter_context(tc.tile_pool(name="shared", bufs=1))
         psum = ctx.enter_context(tc.psum_pool(name="psum", bufs=1))
 
         scale_table = keep.tile([P, T], U8, name="scale_table", align_bytes=64)
@@ -45,7 +46,10 @@ def tile_picked_zlate_max_p_kernel(tc, x_words, x_scales, hT, offs, out):
         h_raw = {}
 
         def load_queries(t, o):
-            h_raw[t, o] = keep.tile([P, PACK, P], F32, name="h_raw%d_%d" % (t, o), align_bytes=64)
+            if (t, o) == (0, 0):
+                h_raw[t, o] = shared.tile([P, PACK, P], F32, name="h_raw0_0", align_bytes=64, offset=0)
+            else:
+                h_raw[t, o] = keep.tile([P, PACK, P], F32, name="h_raw%d_%d" % (t, o), align_bytes=64)
             rows = hT[o * K_PASS : (o + 1) * K_PASS, t * P : (t + 1) * P]
             nc.sync.dma_start(out=h_raw[t, o][:], in_=rows.rearrange("(p j) c -> p j c", j=PACK))
 
@@ -80,17 +84,23 @@ def tile_picked_zlate_max_p_kernel(tc, x_words, x_scales, hT, offs, out):
 
         x_code = {}
 
-        def gather_words(o, h, tag):
-            x_code[o, h] = keep.tile([P, N], U32, name="x_code%d_%d" % (o, h), tag=tag, align_bytes=64)
+        def gather_words(o, h):
+            if (o, h) == (1, 1):
+                x_code[o, h] = shared.tile([P, N], U32, name="x_code1_1", align_bytes=64, offset=4 * P)
+            else:
+                x_code[o, h] = keep.tile([P, N], U32, name="x_code%d_%d" % (o, h), align_bytes=64)
             part = offsets[:, h * LIST_COLS : (h + 1) * LIST_COLS]
             nc.vector.tensor_copy(x_code[o, h][:], word_table[o][:].bitcast(U32).indirect(part))
 
         h_bf, h_code, h_scale, whole = {}, {}, {}, {}
 
-        def group(t, passes, code_tag=None):
+        def group(t, passes):
             name = "%d_%d" % (t, passes[0])
             bf = keep.tile([P, len(passes), P, PACK], BF16, name="h_bf" + name, align_bytes=64)
-            code = keep.tile([P, len(passes) * P], U32, name="h_code" + name, tag=code_tag or "h_code" + name, align_bytes=64)
+            if name == "0_1":
+                code = shared.tile([P, P], U32, name="h_code0_1", align_bytes=64, offset=0)
+            else:
+                code = keep.tile([P, len(passes) * P], U32, name="h_code" + name, align_bytes=64)
             scale = keep.tile([P, len(passes) * P], U8, name="h_scale" + name, align_bytes=64)
             whole[t, passes[0]] = (bf, code, scale)
             for i, o in enumerate(passes):
@@ -128,18 +138,16 @@ def tile_picked_zlate_max_p_kernel(tc, x_words, x_scales, hT, offs, out):
                 stop=(o == PASSES - 1),
             )
 
-        def pool_max(t, h, tag):
-            best = keep.tile([P, DOCS], F32, name="best%d_%d" % (t, h), tag=tag, align_bytes=64)
+        def pool_max(t, h, best):
             nc.vector.tensor_reduce(
-                out=best[:],
+                out=best,
                 in_=bank[t, h][:].rearrange("p (v d) -> p v d", d=D),
                 axis=mybir.AxisListType.X,
                 op=MAX,
             )
-            nc.sync.dma_start(out=out[t * P : (t + 1) * P, h * DOCS : (h + 1) * DOCS], in_=best[:])
+            nc.sync.dma_start(out=out[t * P : (t + 1) * P, h * DOCS : (h + 1) * DOCS], in_=best)
 
-        def tile_max(t, tag):
-            best = keep.tile([P, HALVES, DOCS], F32, name="best%d" % t, tag=tag, align_bytes=64)
+        def tile_max(t, best):
             for h in range(HALVES):
                 nc.vector.tensor_reduce(
                     out=best[:, h],
@@ -147,23 +155,36 @@ def tile_picked_zlate_max_p_kernel(tc, x_words, x_scales, hT, offs, out):
                     axis=mybir.AxisListType.X,
                     op=MAX,
                 )
-            nc.sync.dma_start(out=out[t * P : (t + 1) * P, :], in_=best[:].rearrange("p h v -> p (h v)"))
+            nc.sync.dma_start(out=out[t * P : (t + 1) * P, :], in_=best.rearrange("p h v -> p (h v)"))
+
+        def warm_up():
+            nc.tensor.matmul_mx(
+                out=bank[Q_TILES - 1, HALVES - 1][:],
+                lhsT=x_code[0, 0][:, 0:P].bitcast(FP8X4),
+                lhsT_scale=x_scale[0][:, 0:P],
+                rhs=x_code[0, 0][:].bitcast(FP8X4),
+                rhs_scale=x_scale[0][:, 0:N],
+                start=True,
+                stop=True,
+            )
 
         group(0, [0])
         for t in range(1, Q_TILES):
             group(t, [0, 1])
         for h in range(HALVES):
-            gather_words(0, h, "x_code0_%d" % h)
-        group(0, [1], "h_bf0_0")
+            gather_words(0, h)
+        for n in range(4):
+            warm_up()
+        group(0, [1])
         for t in range(Q_TILES):
             for o in range(PASSES):
                 if (t, o) != (0, 1):
                     interleave(t, o, nc.scalar.copy)
-        gather_words(1, 0, "x_code1_0")
+        gather_words(1, 0)
         interleave(0, 1, nc.vector.tensor_copy)
         quantize(0, 0)
         quantize(0, 1)
-        gather_words(1, 1, "h_bf0_1")
+        gather_words(1, 1)
         for h in range(HALVES):
             for o in range(PASSES):
                 multiply(0, o, h)
@@ -172,9 +193,9 @@ def tile_picked_zlate_max_p_kernel(tc, x_words, x_scales, hT, offs, out):
             for h in range(HALVES):
                 for o in range(PASSES):
                     multiply(t, o, h)
-        tile_max(0, "h_bf1_0")
-        pool_max(1, 0, "h_bf2_0")
-        pool_max(1, 1, "h_bf3_0")
-        tile_max(2, "best2")
-        pool_max(3, 0, "best3_0")
-        pool_max(3, 1, "best3_1")
+        tile_max(0, h_raw[1, 1][:, 0:HALVES])
+        pool_max(1, 0, h_raw[2, 1][:, 0])
+        pool_max(1, 1, h_raw[3, 1][:, 0])
+        tile_max(2, h_raw[3, 1][:, 1 : 1 + HALVES])
+        pool_max(3, 0, h_raw[3, 0][:, 0])
+        pool_max(3, 1, h_raw[3, 0][:, 1])

@@ -169,8 +169,10 @@ def tile_picked_zlate_max_p_kernel(tc, x_words, x_scales, hT, offs, out):
             )
 
         group(0, [0])
-        for t in range(1, Q_TILES):
+        for t in range(1, Q_TILES - 1):
             group(t, [0, 1])
+        group(3, [0])
+        group(3, [1])
         for h in range(HALVES):
             gather_words(0, h)
         for n in range(4):
@@ -188,14 +190,17 @@ def tile_picked_zlate_max_p_kernel(tc, x_words, x_scales, hT, offs, out):
         for h in range(HALVES):
             for o in range(PASSES):
                 multiply(0, o, h)
-        for t in range(1, Q_TILES):
+        for t in range(1, Q_TILES - 1):
             quantize(t, 0)
             for h in range(HALVES):
                 for o in range(PASSES):
                     multiply(t, o, h)
         tile_max(0, h_raw[1, 1][:, 0:HALVES])
-        pool_max(1, 0, h_raw[2, 1][:, 0])
-        pool_max(1, 1, h_raw[3, 1][:, 0])
-        tile_max(2, h_raw[3, 1][:, 1 : 1 + HALVES])
+        tile_max(1, h_raw[2, 1][:, 0:HALVES])
+        for o in range(PASSES):
+            quantize(3, o)
+            for h in range(HALVES):
+                multiply(3, o, h)
+        tile_max(2, h_raw[3, 1][:, 0:HALVES])
         pool_max(3, 0, h_raw[3, 0][:, 0])
         pool_max(3, 1, h_raw[3, 0][:, 1])

@@ -30,7 +30,6 @@ def tile_picked_zlate_max_p_kernel(tc, x_words, x_scales, hT, offs, out):
     nc = tc.nc
     with ExitStack() as ctx:
         keep = ctx.enter_context(tc.tile_pool(name="keep", bufs=1))
-        shared = ctx.enter_context(tc.tile_pool(name="shared", bufs=1))
         psum = ctx.enter_context(tc.psum_pool(name="psum", bufs=1))
 
         scale_table = keep.tile([P, T], U8, name="scale_table", align_bytes=64)
@@ -46,10 +45,7 @@ def tile_picked_zlate_max_p_kernel(tc, x_words, x_scales, hT, offs, out):
         h_raw = {}
 
         def load_queries(t, o):
-            if (t, o) == (0, 0):
-                h_raw[t, o] = shared.tile([P, PACK, P], F32, name="h_raw0_0", align_bytes=64, offset=0)
-            else:
-                h_raw[t, o] = keep.tile([P, PACK, P], F32, name="h_raw%d_%d" % (t, o), align_bytes=64)
+            h_raw[t, o] = keep.tile([P, PACK, P], F32, name="h_raw%d_%d" % (t, o), align_bytes=64)
             rows = hT[o * K_PASS : (o + 1) * K_PASS, t * P : (t + 1) * P]
             nc.sync.dma_start(out=h_raw[t, o][:], in_=rows.rearrange("(p j) c -> p j c", j=PACK))
 
@@ -73,8 +69,8 @@ def tile_picked_zlate_max_p_kernel(tc, x_words, x_scales, hT, offs, out):
                     in_=picked[4 * o + 8 * i : P : 32, :].bitcast(I32),
                 )
             if o == 0:
-                load_words(1, slice(T - HEAD, T))
                 load_queries(0, 0)
+                load_words(1, slice(T - HEAD, T))
                 load_queries(0, 1)
 
         for t in range(Q_TILES):
@@ -85,10 +81,8 @@ def tile_picked_zlate_max_p_kernel(tc, x_words, x_scales, hT, offs, out):
         x_code = {}
 
         def gather_words(o, h):
-            if (o, h) == (1, 1):
-                x_code[o, h] = shared.tile([P, N], U32, name="x_code1_1", align_bytes=64, offset=4 * P)
-            else:
-                x_code[o, h] = keep.tile([P, N], U32, name="x_code%d_%d" % (o, h), align_bytes=64)
+            tag = "h_raw0_%d" % h if o == 1 else "x_code%d_%d" % (o, h)
+            x_code[o, h] = keep.tile([P, N], U32, name="x_code%d_%d" % (o, h), tag=tag, align_bytes=64)
             part = offsets[:, h * LIST_COLS : (h + 1) * LIST_COLS]
             nc.vector.tensor_copy(x_code[o, h][:], word_table[o][:].bitcast(U32).indirect(part))
 
@@ -97,10 +91,7 @@ def tile_picked_zlate_max_p_kernel(tc, x_words, x_scales, hT, offs, out):
         def group(t, passes):
             name = "%d_%d" % (t, passes[0])
             bf = keep.tile([P, len(passes), P, PACK], BF16, name="h_bf" + name, align_bytes=64)
-            if name == "0_1":
-                code = shared.tile([P, P], U32, name="h_code0_1", align_bytes=64, offset=0)
-            else:
-                code = keep.tile([P, len(passes) * P], U32, name="h_code" + name, align_bytes=64)
+            code = keep.tile([P, len(passes) * P], U32, name="h_code" + name, align_bytes=64)
             scale = keep.tile([P, len(passes) * P], U8, name="h_scale" + name, align_bytes=64)
             whole[t, passes[0]] = (bf, code, scale)
             for i, o in enumerate(passes):
@@ -113,10 +104,10 @@ def tile_picked_zlate_max_p_kernel(tc, x_words, x_scales, hT, offs, out):
             for h in range(HALVES):
                 bank[t, h] = psum.tile([P, N], F32, name="bank%d_%d" % (t, h))
 
-        def interleave(t, o, copy):
+        def interleave(t, o, copy, cols=slice(0, P)):
             copy(
-                out=h_bf[t, o].rearrange("p (c i) j -> p c j i", i=4),
-                in_=h_raw[t, o][:].rearrange("p j (c i) -> p c j i", i=4),
+                out=h_bf[t, o][:, cols].rearrange("p (c i) j -> p c j i", i=4),
+                in_=h_raw[t, o][:, :, cols].rearrange("p j (c i) -> p c j i", i=4),
             )
 
         def quantize(t, o):
@@ -157,50 +148,42 @@ def tile_picked_zlate_max_p_kernel(tc, x_words, x_scales, hT, offs, out):
                 )
             nc.sync.dma_start(out=out[t * P : (t + 1) * P, :], in_=best.rearrange("p h v -> p (h v)"))
 
-        def warm_up():
-            nc.tensor.matmul_mx(
-                out=bank[Q_TILES - 1, HALVES - 1][:],
-                lhsT=x_code[0, 0][:, 0:P].bitcast(FP8X4),
-                lhsT_scale=x_scale[0][:, 0:P],
-                rhs=x_code[0, 0][:].bitcast(FP8X4),
-                rhs_scale=x_scale[0][:, 0:N],
-                start=True,
-                stop=True,
-            )
-
         group(0, [0])
-        for t in range(1, Q_TILES - 1):
-            group(t, [0, 1])
+        group(1, [0])
+        group(1, [1])
+        group(2, [0, 1])
         group(3, [0])
         group(3, [1])
         for h in range(HALVES):
             gather_words(0, h)
-        for n in range(4):
-            warm_up()
         group(0, [1])
         for t in range(Q_TILES):
             for o in range(PASSES):
-                if (t, o) != (0, 1):
-                    interleave(t, o, nc.scalar.copy)
+                interleave(t, o, nc.scalar.copy)
+
+        def feed(t, o):
+            quantize(t, o)
+            for h in range(HALVES):
+                multiply(t, o, h)
+
+        feed(0, 0)
         gather_words(1, 0)
-        interleave(0, 1, nc.vector.tensor_copy)
-        quantize(0, 0)
         quantize(0, 1)
+        multiply(0, 1, 0)
         gather_words(1, 1)
+        multiply(0, 1, 1)
+        feed(1, 0)
+        pool_max(0, 0, h_raw[1, 0][:, 0])
+        feed(1, 1)
+        pool_max(0, 1, h_raw[1, 1][:, 0])
+        quantize(2, 0)
         for h in range(HALVES):
             for o in range(PASSES):
-                multiply(0, o, h)
-        for t in range(1, Q_TILES - 1):
-            quantize(t, 0)
-            for h in range(HALVES):
-                for o in range(PASSES):
-                    multiply(t, o, h)
-        tile_max(0, h_raw[1, 1][:, 0:HALVES])
-        tile_max(1, h_raw[2, 1][:, 0:HALVES])
-        for o in range(PASSES):
-            quantize(3, o)
-            for h in range(HALVES):
-                multiply(3, o, h)
+                multiply(2, o, h)
+        pool_max(1, 0, h_raw[2, 1][:, 0])
+        feed(3, 0)
+        pool_max(1, 1, h_raw[3, 0][:, 0])
+        feed(3, 1)
         tile_max(2, h_raw[3, 1][:, 0:HALVES])
-        pool_max(3, 0, h_raw[3, 0][:, 0])
-        pool_max(3, 1, h_raw[3, 0][:, 1])
+        pool_max(3, 0, h_raw[3, 0][:, 1])
+        pool_max(3, 1, h_raw[3, 0][:, 2])

@@ -24,6 +24,7 @@ Q_TILES = J // P
 LIST_COLS = N // 16
 DOCS = N // D
 HEAD = 1024
+TAIL = 1024
 
 
 def tile_picked_zlate_max_p_kernel(tc, x_words, x_scales, hT, offs, out):
@@ -56,7 +57,7 @@ def tile_picked_zlate_max_p_kernel(tc, x_words, x_scales, hT, offs, out):
             in_=x_scales.rearrange("o m c -> m o c").bitcast(I32),
         )
         load_words(0, slice(HEAD, T))
-        load_words(1, slice(0, T - HEAD))
+        load_words(1, slice(0, T - TAIL))
 
         picked = keep.tile([P, S], U8, name="picked", align_bytes=64)
         x_scale = [keep.tile([P, S], U8, name="x_scale%d" % o, align_bytes=64) for o in range(PASSES)]
@@ -70,8 +71,9 @@ def tile_picked_zlate_max_p_kernel(tc, x_words, x_scales, hT, offs, out):
                 )
             if o == 0:
                 load_queries(0, 0)
-                load_words(1, slice(T - HEAD, T))
+                load_words(1, slice(T - TAIL, T))
                 load_queries(0, 1)
+                load_queries(1, 0)
 
         for t in range(Q_TILES):
             for o in range(PASSES):
@@ -91,7 +93,8 @@ def tile_picked_zlate_max_p_kernel(tc, x_words, x_scales, hT, offs, out):
         def group(t, passes):
             name = "%d_%d" % (t, passes[0])
             bf = keep.tile([P, len(passes), P, PACK], BF16, name="h_bf" + name, align_bytes=64)
-            code = keep.tile([P, len(passes) * P], U32, name="h_code" + name, align_bytes=64)
+            tag = "picked" if (t, passes[0]) == (1, 0) else "h_code" + name
+            code = keep.tile([P, len(passes) * P], U32, name="h_code" + name, tag=tag, align_bytes=64)
             scale = keep.tile([P, len(passes) * P], U8, name="h_scale" + name, align_bytes=64)
             whole[t, passes[0]] = (bf, code, scale)
             for i, o in enumerate(passes):
@@ -151,7 +154,8 @@ def tile_picked_zlate_max_p_kernel(tc, x_words, x_scales, hT, offs, out):
         group(0, [0])
         group(1, [0])
         group(1, [1])
-        group(2, [0, 1])
+        group(2, [0])
+        group(2, [1])
         group(3, [0])
         group(3, [1])
         for h in range(HALVES):
@@ -176,10 +180,8 @@ def tile_picked_zlate_max_p_kernel(tc, x_words, x_scales, hT, offs, out):
         pool_max(0, 0, h_raw[1, 0][:, 0])
         feed(1, 1)
         pool_max(0, 1, h_raw[1, 1][:, 0])
-        quantize(2, 0)
-        for h in range(HALVES):
-            for o in range(PASSES):
-                multiply(2, o, h)
+        feed(2, 0)
+        feed(2, 1)
         pool_max(1, 0, h_raw[2, 1][:, 0])
         feed(3, 0)
         pool_max(1, 1, h_raw[3, 0][:, 0])

@@ -15,16 +15,15 @@ FP8X4 = mybir.dt.float8_e4m3fn_x4
 MAX = mybir.AluOpType.max
 
 P = 128
+QUAD = 32
 PACK = 4
 K_PASS = P * PACK
 PASSES = K // K_PASS
 N = 512
 HALVES = S // N
 Q_TILES = J // P
-LIST_COLS = N // 16
 DOCS = N // D
 HEAD = 1024
-TAIL = 1024
 
 
 def tile_picked_zlate_max_p_kernel(tc, x_words, x_scales, hT, offs, out):
@@ -35,6 +34,8 @@ def tile_picked_zlate_max_p_kernel(tc, x_words, x_scales, hT, offs, out):
 
         scale_table = keep.tile([P, T], U8, name="scale_table", align_bytes=64)
         nc.vector.memset(scale_table[:].bitcast(I32), 0)
+        x_scale = keep.tile([P, PASSES * S], U8, name="x_scale", align_bytes=64)
+        nc.vector.memset(x_scale[:].bitcast(I32), 0)
 
         word_table = [keep.tile([P, T], I32, name="word_table%d" % o, align_bytes=64) for o in range(PASSES)]
         offsets = keep.tile([P, S // 16], U16, name="offsets")
@@ -57,79 +58,64 @@ def tile_picked_zlate_max_p_kernel(tc, x_words, x_scales, hT, offs, out):
             in_=x_scales.rearrange("o m c -> m o c").bitcast(I32),
         )
         load_words(0, slice(HEAD, T))
-        load_words(1, slice(0, T - TAIL))
+        load_words(1, slice(0, T))
 
         picked = keep.tile([P, S], U8, name="picked", align_bytes=64)
-        x_scale = [keep.tile([P, S], U8, name="x_scale%d" % o, align_bytes=64) for o in range(PASSES)]
         nc.vector.tensor_copy(picked[:], scale_table[:].indirect(offsets[:]))
-        for o in range(PASSES):
-            nc.vector.tensor_copy(x_scale[o][:].bitcast(I32), picked[:].bitcast(I32))
-            for i in range(1, 4):
-                nc.sync.dma_start(
-                    out=x_scale[o][4 * o + i : P : 32, :].bitcast(I32),
-                    in_=picked[4 * o + 8 * i : P : 32, :].bitcast(I32),
-                )
-            if o == 0:
-                load_queries(0, 0)
-                load_words(1, slice(T - TAIL, T))
-                load_queries(0, 1)
-                load_queries(1, 0)
 
-        for t in range(Q_TILES):
+        for o in range(PASSES):
+            load_queries(0, o)
+        for q in range(0, P, QUAD):
+            nc.sync.dma_start(
+                out=x_scale[q : q + 4, :].bitcast(I32).rearrange("p (o c) -> p o c", o=PASSES),
+                in_=picked[q : q + QUAD : 4, :].bitcast(I32),
+            )
+        for t in range(1, Q_TILES):
             for o in range(PASSES):
-                if (t, o) not in h_raw:
-                    load_queries(t, o)
+                load_queries(t, o)
 
         x_code = {}
 
-        def gather_words(o, h):
-            tag = "h_raw0_%d" % h if o == 1 else "x_code%d_%d" % (o, h)
-            x_code[o, h] = keep.tile([P, N], U32, name="x_code%d_%d" % (o, h), tag=tag, align_bytes=64)
-            part = offsets[:, h * LIST_COLS : (h + 1) * LIST_COLS]
-            nc.vector.tensor_copy(x_code[o, h][:], word_table[o][:].bitcast(U32).indirect(part))
+        def gather_words(o, first, count, tag=None):
+            name = "x_code%d_%d" % (o, first)
+            x_code[o, first] = keep.tile([P, count], U32, name=name, tag=tag or name, align_bytes=64)
+            part = offsets[:, first // 16 : (first + count) // 16]
+            nc.vector.tensor_copy(x_code[o, first][:], word_table[o][:].bitcast(U32).indirect(part))
 
-        h_bf, h_code, h_scale, whole = {}, {}, {}, {}
-
-        def group(t, passes):
-            name = "%d_%d" % (t, passes[0])
-            bf = keep.tile([P, len(passes), P, PACK], BF16, name="h_bf" + name, align_bytes=64)
-            tag = "picked" if (t, passes[0]) == (1, 0) else "h_code" + name
-            code = keep.tile([P, len(passes) * P], U32, name="h_code" + name, tag=tag, align_bytes=64)
-            scale = keep.tile([P, len(passes) * P], U8, name="h_scale" + name, align_bytes=64)
-            whole[t, passes[0]] = (bf, code, scale)
-            for i, o in enumerate(passes):
-                h_bf[t, o] = bf[:, i]
-                h_code[t, o] = code[:, i * P : (i + 1) * P]
-                h_scale[t, o] = scale[:, i * P : (i + 1) * P]
-
+        h_bf, h_code, h_scale = {}, {}, {}
         bank = {}
         for t in range(Q_TILES):
             for h in range(HALVES):
                 bank[t, h] = psum.tile([P, N], F32, name="bank%d_%d" % (t, h))
 
-        def interleave(t, o, copy, cols=slice(0, P)):
-            copy(
-                out=h_bf[t, o][:, cols].rearrange("p (c i) j -> p c j i", i=4),
-                in_=h_raw[t, o][:, :, cols].rearrange("p j (c i) -> p c j i", i=4),
+        def interleave(t, o):
+            h_bf[t, o] = keep.tile([P, P, PACK], BF16, name="h_bf%d_%d" % (t, o), align_bytes=64)
+            nc.scalar.copy(
+                out=h_bf[t, o][:].rearrange("p (c i) j -> p c j i", i=4),
+                in_=h_raw[t, o][:].rearrange("p j (c i) -> p c j i", i=4),
             )
 
         def quantize(t, o):
-            bf, code, scale = whole[t, o]
+            tag = "h_code%d_%d" % (t % (PASSES - o), o)
+            h_code[t, o] = keep.tile([P, P], U32, name="h_code%d_%d" % (t, o), tag=tag, align_bytes=64)
+            h_scale[t, o] = keep.tile([P, P], U8, name="h_scale%d_%d" % (t, o), align_bytes=64)
             nc.vector.quantize_mx(
-                out=code[:].bitcast(FP8X4),
-                scales=scale[:],
-                in_=bf[:].rearrange("p i c j -> p (i c j)"),
+                out=h_code[t, o][:].bitcast(FP8X4),
+                scales=h_scale[t, o][:],
+                in_=h_bf[t, o][:].rearrange("p c j -> p (c j)"),
             )
 
-        def multiply(t, o, h):
+        def multiply(t, o, first, start, stop):
+            count = x_code[o, first].shape[1]
+            col = first % N
             nc.tensor.matmul_mx(
-                out=bank[t, h][:],
-                lhsT=h_code[t, o].bitcast(FP8X4),
-                lhsT_scale=h_scale[t, o],
-                rhs=x_code[o, h][:].bitcast(FP8X4),
-                rhs_scale=x_scale[o][4 * o : P, h * N : (h + 1) * N],
-                start=(o == 0),
-                stop=(o == PASSES - 1),
+                out=bank[t, first // N][:, col : col + count],
+                lhsT=h_code[t, o][:].bitcast(FP8X4),
+                lhsT_scale=h_scale[t, o][:],
+                rhs=x_code[o, first][:].bitcast(FP8X4),
+                rhs_scale=x_scale[:, o * S + first : o * S + first + count],
+                start=start,
+                stop=stop,
             )
 
         def pool_max(t, h, best):
@@ -141,51 +127,35 @@ def tile_picked_zlate_max_p_kernel(tc, x_words, x_scales, hT, offs, out):
             )
             nc.sync.dma_start(out=out[t * P : (t + 1) * P, h * DOCS : (h + 1) * DOCS], in_=best)
 
-        def tile_max(t, best):
-            for h in range(HALVES):
-                nc.vector.tensor_reduce(
-                    out=best[:, h],
-                    in_=bank[t, h][:].rearrange("p (v d) -> p v d", d=D),
-                    axis=mybir.AxisListType.X,
-                    op=MAX,
-                )
-            nc.sync.dma_start(out=out[t * P : (t + 1) * P, :], in_=best.rearrange("p h v -> p (h v)"))
-
-        group(0, [0])
-        group(1, [0])
-        group(1, [1])
-        group(2, [0])
-        group(2, [1])
-        group(3, [0])
-        group(3, [1])
         for h in range(HALVES):
-            gather_words(0, h)
-        group(0, [1])
+            gather_words(0, h * N, N)
+        gather_words(1, 0, N)
         for t in range(Q_TILES):
             for o in range(PASSES):
-                interleave(t, o, nc.scalar.copy)
+                interleave(t, o)
 
-        def feed(t, o):
-            quantize(t, o)
-            for h in range(HALVES):
-                multiply(t, o, h)
-
-        feed(0, 0)
-        gather_words(1, 0)
+        quantize(0, 0)
+        multiply(0, 0, 0, True, False)
+        gather_words(1, N, N // 2, "h_raw0_0")
         quantize(0, 1)
-        multiply(0, 1, 0)
-        gather_words(1, 1)
-        multiply(0, 1, 1)
-        feed(1, 0)
-        pool_max(0, 0, h_raw[1, 0][:, 0])
-        feed(1, 1)
-        pool_max(0, 1, h_raw[1, 1][:, 0])
-        feed(2, 0)
-        feed(2, 1)
-        pool_max(1, 0, h_raw[2, 1][:, 0])
-        feed(3, 0)
-        pool_max(1, 1, h_raw[3, 0][:, 0])
-        feed(3, 1)
-        tile_max(2, h_raw[3, 1][:, 0:HALVES])
-        pool_max(3, 0, h_raw[3, 0][:, 1])
-        pool_max(3, 1, h_raw[3, 0][:, 2])
+        multiply(0, 1, 0, False, True)
+        multiply(0, 1, N, True, False)
+        gather_words(1, N + N // 2, N // 2, "h_raw0_1")
+        multiply(0, 1, N + N // 2, False, False)
+        multiply(0, 0, N, False, True)
+        for t in range(1, Q_TILES):
+            quantize(t, 0)
+            last = t == Q_TILES - 1
+            multiply(t, 0, 0, True, False)
+            if last:
+                multiply(t, 0, N, True, False)
+            pool_max(t - 1, 0, h_raw[t, 0][:, 0])
+            quantize(t, 1)
+            multiply(t, 1, 0, False, True)
+            multiply(t, 1, N, not last, False)
+            multiply(t, 1, N + N // 2, False, last)
+            if not last:
+                multiply(t, 0, N, False, True)
+            pool_max(t - 1, 1, h_raw[t, 1][:, 0])
+        for h in range(HALVES):
+            pool_max(Q_TILES - 1, h, h_raw[Q_TILES - 1, 0][:, 1 + h])

@@ -32,12 +32,12 @@ def tile_picked_zlate_max_p_kernel(tc, x_words, x_scales, hT, offs, out):
         keep = ctx.enter_context(tc.tile_pool(name="keep", bufs=1))
         psum = ctx.enter_context(tc.psum_pool(name="psum", bufs=1))
 
-        scale_table = keep.tile([P, T], U8, name="scale_table", align_bytes=64)
+        scale_table = keep.tile([P, T], U8, name="scale_table", align_bytes=256)
         nc.vector.memset(scale_table[:].bitcast(I32), 0)
-        x_scale = keep.tile([P, PASSES * S], U8, name="x_scale", align_bytes=64)
+        x_scale = keep.tile([P, PASSES * S], U8, name="x_scale", align_bytes=256)
         nc.vector.memset(x_scale[:].bitcast(I32), 0)
 
-        word_table = [keep.tile([P, T], I32, name="word_table%d" % o, align_bytes=64) for o in range(PASSES)]
+        word_table = [keep.tile([P, T], I32, name="word_table%d" % o, align_bytes=256) for o in range(PASSES)]
         offsets = keep.tile([P, S // 16], U16, name="offsets")
 
         def load_words(o, cols):
@@ -47,7 +47,7 @@ def tile_picked_zlate_max_p_kernel(tc, x_words, x_scales, hT, offs, out):
         h_raw = {}
 
         def load_queries(t, o):
-            h_raw[t, o] = keep.tile([P, PACK, P], F32, name="h_raw%d_%d" % (t, o), align_bytes=64)
+            h_raw[t, o] = keep.tile([P, PACK, P], F32, name="h_raw%d_%d" % (t, o), align_bytes=256)
             rows = hT[o * K_PASS : (o + 1) * K_PASS, t * P : (t + 1) * P]
             nc.sync.dma_start(out=h_raw[t, o][:], in_=rows.rearrange("(p j) c -> p j c", j=PACK))
 
@@ -60,25 +60,26 @@ def tile_picked_zlate_max_p_kernel(tc, x_words, x_scales, hT, offs, out):
         load_words(0, slice(HEAD, T))
         load_words(1, slice(0, T))
 
-        picked = keep.tile([P, S], U8, name="picked", align_bytes=64)
+        picked = keep.tile([P, S], U8, name="picked", align_bytes=256)
         nc.vector.tensor_copy(picked[:], scale_table[:].indirect(offsets[:]))
 
         for o in range(PASSES):
             load_queries(0, o)
-        for q in range(0, P, QUAD):
+        for q in (0, 2 * QUAD, QUAD, 3 * QUAD):
             nc.sync.dma_start(
                 out=x_scale[q : q + 4, :].bitcast(I32).rearrange("p (o c) -> p o c", o=PASSES),
                 in_=picked[q : q + QUAD : 4, :].bitcast(I32),
             )
-        for t in range(1, Q_TILES):
+        for t in range(Q_TILES):
             for o in range(PASSES):
-                load_queries(t, o)
+                if (t, o) not in h_raw:
+                    load_queries(t, o)
 
         x_code = {}
 
         def gather_words(o, first, count, tag=None):
             name = "x_code%d_%d" % (o, first)
-            x_code[o, first] = keep.tile([P, count], U32, name=name, tag=tag or name, align_bytes=64)
+            x_code[o, first] = keep.tile([P, count], U32, name=name, tag=tag or name, align_bytes=256)
             part = offsets[:, first // 16 : (first + count) // 16]
             nc.vector.tensor_copy(x_code[o, first][:], word_table[o][:].bitcast(U32).indirect(part))
 
@@ -89,30 +90,30 @@ def tile_picked_zlate_max_p_kernel(tc, x_words, x_scales, hT, offs, out):
                 bank[t, h] = psum.tile([P, N], F32, name="bank%d_%d" % (t, h))
 
         def interleave(t, o):
-            h_bf[t, o] = keep.tile([P, P, PACK], BF16, name="h_bf%d_%d" % (t, o), align_bytes=64)
+            h_bf[t, o] = keep.tile([P, P, PACK], BF16, name="h_bf%d_%d" % (t, o), align_bytes=256)
             nc.scalar.copy(
                 out=h_bf[t, o][:].rearrange("p (c i) j -> p c j i", i=4),
                 in_=h_raw[t, o][:].rearrange("p j (c i) -> p c j i", i=4),
             )
 
         def quantize(t, o):
-            tag = "h_code%d_%d" % (t % (PASSES - o), o)
-            h_code[t, o] = keep.tile([P, P], U32, name="h_code%d_%d" % (t, o), tag=tag, align_bytes=64)
-            h_scale[t, o] = keep.tile([P, P], U8, name="h_scale%d_%d" % (t, o), align_bytes=64)
+            h_code[t, o] = keep.tile([P, P], U32, name="h_code%d_%d" % (t, o), align_bytes=256)
+            h_scale[t, o] = keep.tile([P, P], U8, name="h_scale%d_%d" % (t, o), align_bytes=256)
             nc.vector.quantize_mx(
                 out=h_code[t, o][:].bitcast(FP8X4),
                 scales=h_scale[t, o][:],
                 in_=h_bf[t, o][:].rearrange("p c j -> p (c j)"),
             )
 
-        def multiply(t, o, first, start, stop):
-            count = x_code[o, first].shape[1]
+        def multiply(t, o, first, start, stop, count=None):
+            base = max(f for which, f in x_code if which == o and f <= first)
+            count = count or x_code[o, base].shape[1]
             col = first % N
             nc.tensor.matmul_mx(
                 out=bank[t, first // N][:, col : col + count],
                 lhsT=h_code[t, o][:].bitcast(FP8X4),
                 lhsT_scale=h_scale[t, o][:],
-                rhs=x_code[o, first][:].bitcast(FP8X4),
+                rhs=x_code[o, base][:, first - base : first - base + count].bitcast(FP8X4),
                 rhs_scale=x_scale[:, o * S + first : o * S + first + count],
                 start=start,
                 stop=stop,
@@ -136,26 +137,35 @@ def tile_picked_zlate_max_p_kernel(tc, x_words, x_scales, hT, offs, out):
 
         quantize(0, 0)
         multiply(0, 0, 0, True, False)
+        multiply(0, 0, N, True, False, N // 2)
         gather_words(1, N, N // 2, "h_raw0_0")
         quantize(0, 1)
         multiply(0, 1, 0, False, True)
-        multiply(0, 1, N, True, False)
+        multiply(0, 1, N, False, False)
+        multiply(0, 0, N + N // 2, False, False, N // 2)
         gather_words(1, N + N // 2, N // 2, "h_raw0_1")
-        multiply(0, 1, N + N // 2, False, False)
-        multiply(0, 0, N, False, True)
-        for t in range(1, Q_TILES):
-            quantize(t, 0)
-            last = t == Q_TILES - 1
-            multiply(t, 0, 0, True, False)
-            if last:
+        multiply(0, 1, N + N // 2, False, True)
+
+        def feed(t, o):
+            quantize(t, o)
+            if o == 0:
+                multiply(t, 0, 0, True, False)
                 multiply(t, 0, N, True, False)
-            pool_max(t - 1, 0, h_raw[t, 0][:, 0])
-            quantize(t, 1)
-            multiply(t, 1, 0, False, True)
-            multiply(t, 1, N, not last, False)
-            multiply(t, 1, N + N // 2, False, last)
-            if not last:
-                multiply(t, 0, N, False, True)
-            pool_max(t - 1, 1, h_raw[t, 1][:, 0])
-        for h in range(HALVES):
-            pool_max(Q_TILES - 1, h, h_raw[Q_TILES - 1, 0][:, 1 + h])
+            else:
+                multiply(t, 1, 0, False, True)
+                multiply(t, 1, N, False, False)
+                multiply(t, 1, N + N // 2, False, True)
+
+        feed(1, 0)
+        pool_max(0, 0, h_raw[1, 0][:, 0])
+        feed(1, 1)
+        feed(2, 0)
+        pool_max(0, 1, h_raw[2, 0][:, 0])
+        feed(2, 1)
+        pool_max(1, 0, h_raw[2, 1][:, 0])
+        feed(3, 0)
+        pool_max(1, 1, h_raw[3, 0][:, 0])
+        feed(3, 1)
+        for t in (2, 3):
+            for h in range(HALVES):
+                pool_max(t, h, h_raw[3, 1][:, 2 * (t - 2) + h])

@@ -15,7 +15,6 @@ FP8X4 = mybir.dt.float8_e4m3fn_x4
 MAX = mybir.AluOpType.max
 
 P = 128
-QUAD = 32
 PACK = 4
 K_PASS = P * PACK
 PASSES = K // K_PASS
@@ -23,7 +22,9 @@ N = 512
 HALVES = S // N
 Q_TILES = J // P
 DOCS = N // D
+ALIGN = 256
 HEAD = 1024
+TAIL = 1024
 
 
 def tile_picked_zlate_max_p_kernel(tc, x_words, x_scales, hT, offs, out):
@@ -32,135 +33,148 @@ def tile_picked_zlate_max_p_kernel(tc, x_words, x_scales, hT, offs, out):
         keep = ctx.enter_context(tc.tile_pool(name="keep", bufs=1))
         psum = ctx.enter_context(tc.psum_pool(name="psum", bufs=1))
 
-        scale_table = keep.tile([P, T], U8, name="scale_table", align_bytes=256)
-        nc.vector.memset(scale_table[:].bitcast(I32), 0)
-        x_scale = keep.tile([P, PASSES * S], U8, name="x_scale", align_bytes=256)
-        nc.vector.memset(x_scale[:].bitcast(I32), 0)
+        def tile(shape, dtype, name, over=None):
+            return keep.tile(shape, dtype, name=name, tag=over or name, align_bytes=ALIGN)
 
-        word_table = [keep.tile([P, T], I32, name="word_table%d" % o, align_bytes=256) for o in range(PASSES)]
+        scale_table = tile([P, T], U8, "scale_table")
+        nc.vector.memset(scale_table[:].bitcast(I32), 0)
+
+        word_table = [tile([P, T], I32, "word_table%d" % o) for o in range(PASSES)]
         offsets = keep.tile([P, S // 16], U16, name="offsets")
+        picked = tile([P, S], U8, "picked")
+        x_scale = [tile([P, S], U8, "x_scale%d" % o) for o in range(PASSES)]
+        h_raw, h_bf, h_code, h_scale, x_code, bank = {}, {}, {}, {}, {}, {}
 
         def load_words(o, cols):
             words = x_words[o].rearrange("p n t -> p (n t)").bitcast(I32)
             nc.sync.dma_start(out=word_table[o][:, cols], in_=words[:, cols])
 
-        h_raw = {}
+        def load_scales():
+            nc.sync.dma_start(
+                out=scale_table[0:P:4, :].bitcast(I32),
+                in_=x_scales.rearrange("o m c -> m o c").bitcast(I32),
+            )
 
         def load_queries(t, o):
-            h_raw[t, o] = keep.tile([P, PACK, P], F32, name="h_raw%d_%d" % (t, o), align_bytes=256)
+            h_raw[t, o] = tile([P, PACK, P], F32, "h_raw%d_%d" % (t, o))
             rows = hT[o * K_PASS : (o + 1) * K_PASS, t * P : (t + 1) * P]
             nc.sync.dma_start(out=h_raw[t, o][:], in_=rows.rearrange("(p j) c -> p j c", j=PACK))
 
+        def make_plane(o):
+            nc.vector.tensor_copy(x_scale[o][:].bitcast(I32), picked[:].bitcast(I32))
+            for i in range(1, 4):
+                nc.sync.dma_start(
+                    out=x_scale[o][4 * o + i : P : 32, :].bitcast(I32),
+                    in_=picked[4 * o + 8 * i : P : 32, :].bitcast(I32),
+                )
+
         load_words(0, slice(0, HEAD))
         nc.sync.dma_start(offsets[:], offs)
-        nc.sync.dma_start(
-            out=scale_table[0:P:4, :].bitcast(I32),
-            in_=x_scales.rearrange("o m c -> m o c").bitcast(I32),
-        )
+        load_scales()
         load_words(0, slice(HEAD, T))
-        load_words(1, slice(0, T))
-
-        picked = keep.tile([P, S], U8, name="picked", align_bytes=256)
+        load_words(1, slice(0, T - TAIL))
         nc.vector.tensor_copy(picked[:], scale_table[:].indirect(offsets[:]))
+        make_plane(0)
+        load_words(1, slice(T - TAIL, T))
+        load_queries(0, 0)
+        load_queries(0, 1)
+        make_plane(1)
 
-        for o in range(PASSES):
-            load_queries(0, o)
-        for q in (0, 2 * QUAD, QUAD, 3 * QUAD):
-            nc.sync.dma_start(
-                out=x_scale[q : q + 4, :].bitcast(I32).rearrange("p (o c) -> p o c", o=PASSES),
-                in_=picked[q : q + QUAD : 4, :].bitcast(I32),
-            )
         for t in range(Q_TILES):
             for o in range(PASSES):
                 if (t, o) not in h_raw:
                     load_queries(t, o)
 
-        x_code = {}
-
-        def gather_words(o, first, count, tag=None):
-            name = "x_code%d_%d" % (o, first)
-            x_code[o, first] = keep.tile([P, count], U32, name=name, tag=tag or name, align_bytes=256)
-            part = offsets[:, first // 16 : (first + count) // 16]
-            nc.vector.tensor_copy(x_code[o, first][:], word_table[o][:].bitcast(U32).indirect(part))
-
-        h_bf, h_code, h_scale = {}, {}, {}
-        bank = {}
         for t in range(Q_TILES):
             for h in range(HALVES):
                 bank[t, h] = psum.tile([P, N], F32, name="bank%d_%d" % (t, h))
 
+        def gather_words(o, first, count, over=None):
+            x_code[o, first] = tile([P, count], U32, "x_code%d_%d" % (o, first), over)
+            part = offsets[:, first // 16 : (first + count) // 16]
+            nc.vector.tensor_copy(x_code[o, first][:], word_table[o][:].bitcast(U32).indirect(part))
+
         def interleave(t, o):
-            h_bf[t, o] = keep.tile([P, P, PACK], BF16, name="h_bf%d_%d" % (t, o), align_bytes=256)
+            h_bf[t, o] = tile([P, P, PACK], BF16, "h_bf%d_%d" % (t, o))
             nc.scalar.copy(
                 out=h_bf[t, o][:].rearrange("p (c i) j -> p c j i", i=4),
                 in_=h_raw[t, o][:].rearrange("p j (c i) -> p c j i", i=4),
             )
 
-        def quantize(t, o):
-            h_code[t, o] = keep.tile([P, P], U32, name="h_code%d_%d" % (t, o), align_bytes=256)
-            h_scale[t, o] = keep.tile([P, P], U8, name="h_scale%d_%d" % (t, o), align_bytes=256)
+        def quantize(t, o, over=None):
+            h_code[t, o] = tile([P, P], U32, "h_code%d_%d" % (t, o), over)
+            h_scale[t, o] = tile([P, P], U8, "h_scale%d_%d" % (t, o))
             nc.vector.quantize_mx(
                 out=h_code[t, o][:].bitcast(FP8X4),
                 scales=h_scale[t, o][:],
                 in_=h_bf[t, o][:].rearrange("p c j -> p (c j)"),
             )
 
-        def multiply(t, o, first, start, stop, count=None):
-            base = max(f for which, f in x_code if which == o and f <= first)
-            count = count or x_code[o, base].shape[1]
-            col = first % N
+        columns_done = {key: 0 for key in bank}
+
+        def multiply(t, o, first):
+            count = x_code[o, first].shape[1]
+            h, col = divmod(first, N)
+            before = columns_done[t, h]
+            columns_done[t, h] = before + count
             nc.tensor.matmul_mx(
-                out=bank[t, first // N][:, col : col + count],
+                out=bank[t, h][:, col : col + count],
                 lhsT=h_code[t, o][:].bitcast(FP8X4),
                 lhsT_scale=h_scale[t, o][:],
-                rhs=x_code[o, base][:, first - base : first - base + count].bitcast(FP8X4),
-                rhs_scale=x_scale[:, o * S + first : o * S + first + count],
-                start=start,
-                stop=stop,
+                rhs=x_code[o, first][:].bitcast(FP8X4),
+                rhs_scale=x_scale[o][4 * o : P, first : first + count],
+                start=before == 0,
+                stop=before + count == PASSES * N,
             )
 
+        def feed(t, o, over=None):
+            quantize(t, o, over)
+            for first in sorted(f for which, f in x_code if which == o):
+                multiply(t, o, first)
+
+        def tokens(t, h):
+            return bank[t, h][:].rearrange("p (v d) -> p v d", d=D)
+
+        def bank_max(t, h, best):
+            nc.vector.tensor_reduce(out=best, in_=tokens(t, h), axis=mybir.AxisListType.X, op=MAX)
+
+        def store(t, docs, best):
+            nc.sync.dma_start(out=out[t * P : (t + 1) * P, docs], in_=best)
+
         def pool_max(t, h, best):
-            nc.vector.tensor_reduce(
-                out=best,
-                in_=bank[t, h][:].rearrange("p (v d) -> p v d", d=D),
-                axis=mybir.AxisListType.X,
-                op=MAX,
-            )
-            nc.sync.dma_start(out=out[t * P : (t + 1) * P, h * DOCS : (h + 1) * DOCS], in_=best)
+            bank_max(t, h, best)
+            store(t, slice(h * DOCS, (h + 1) * DOCS), best)
 
         for h in range(HALVES):
             gather_words(0, h * N, N)
-        gather_words(1, 0, N)
-        for t in range(Q_TILES):
-            for o in range(PASSES):
-                interleave(t, o)
+        for piece in h_raw:
+            interleave(*piece)
 
+        for step in range(4):
+            nc.tensor.matmul_mx(
+                out=bank[Q_TILES - 1, 1][0:32, :],
+                lhsT=x_code[0, 0][:, 0:32].bitcast(FP8X4),
+                lhsT_scale=x_scale[0][:, 0:32],
+                rhs=x_code[0, 0][:].bitcast(FP8X4),
+                rhs_scale=x_scale[0][:, 0:N],
+                start=True,
+                stop=True,
+            )
+        gather_words(1, 0, N)
         quantize(0, 0)
-        multiply(0, 0, 0, True, False)
-        multiply(0, 0, N, True, False, N // 2)
+        multiply(0, 0, 0)
+        multiply(0, 0, N)
         gather_words(1, N, N // 2, "h_raw0_0")
         quantize(0, 1)
-        multiply(0, 1, 0, False, True)
-        multiply(0, 1, N, False, False)
-        multiply(0, 0, N + N // 2, False, False, N // 2)
+        multiply(0, 1, 0)
+        multiply(0, 1, N)
         gather_words(1, N + N // 2, N // 2, "h_raw0_1")
-        multiply(0, 1, N + N // 2, False, True)
-
-        def feed(t, o):
-            quantize(t, o)
-            if o == 0:
-                multiply(t, 0, 0, True, False)
-                multiply(t, 0, N, True, False)
-            else:
-                multiply(t, 1, 0, False, True)
-                multiply(t, 1, N, False, False)
-                multiply(t, 1, N + N // 2, False, True)
-
-        feed(1, 0)
+        multiply(0, 1, N + N // 2)
+        feed(1, 0, "picked")
         pool_max(0, 0, h_raw[1, 0][:, 0])
         feed(1, 1)
+        pool_max(0, 1, h_raw[1, 1][:, 0])
         feed(2, 0)
-        pool_max(0, 1, h_raw[2, 0][:, 0])
         feed(2, 1)
         pool_max(1, 0, h_raw[2, 1][:, 0])
         feed(3, 0)

@@ -170,15 +170,15 @@ def tile_picked_zlate_max_p_kernel(tc, x_words, x_scales, hT, offs, out):
         multiply(0, 1, N)
         gather_words(1, N + N // 2, N // 2, "h_raw0_1")
         multiply(0, 1, N + N // 2)
-        feed(1, 0, "picked")
+        feed(1, 0)
         pool_max(0, 0, h_raw[1, 0][:, 0])
         feed(1, 1)
         pool_max(0, 1, h_raw[1, 1][:, 0])
         feed(2, 0)
+        pool_max(1, 0, h_raw[2, 0][:, 0])
         feed(2, 1)
-        pool_max(1, 0, h_raw[2, 1][:, 0])
+        pool_max(1, 1, h_raw[2, 1][:, 0])
         feed(3, 0)
-        pool_max(1, 1, h_raw[3, 0][:, 0])
         feed(3, 1)
         for t in (2, 3):
             for h in range(HALVES):

@@ -60,13 +60,11 @@ def tile_picked_zlate_max_p_kernel(tc, x_words, x_scales, hT, offs, out):
             rows = hT[o * K_PASS : (o + 1) * K_PASS, t * P : (t + 1) * P]
             nc.sync.dma_start(out=h_raw[t, o][:], in_=rows.rearrange("(p j) c -> p j c", j=PACK))
 
-        def make_plane(o):
-            nc.vector.tensor_copy(x_scale[o][:].bitcast(I32), picked[:].bitcast(I32))
-            for i in range(1, 4):
-                nc.sync.dma_start(
-                    out=x_scale[o][4 * o + i : P : 32, :].bitcast(I32),
-                    in_=picked[4 * o + 8 * i : P : 32, :].bitcast(I32),
-                )
+        def move_rows(o, i):
+            nc.sync.dma_start(
+                out=x_scale[o][4 * o + i : P : 32, :].bitcast(I32),
+                in_=picked[4 * o + 8 * i : P : 32, :].bitcast(I32),
+            )
 
         load_words(0, slice(0, HEAD))
         nc.sync.dma_start(offsets[:], offs)
@@ -74,11 +72,16 @@ def tile_picked_zlate_max_p_kernel(tc, x_words, x_scales, hT, offs, out):
         load_words(0, slice(HEAD, T))
         load_words(1, slice(0, T - TAIL))
         nc.vector.tensor_copy(picked[:], scale_table[:].indirect(offsets[:]))
-        make_plane(0)
+        for o in range(PASSES):
+            nc.vector.tensor_copy(x_scale[o][:].bitcast(I32), picked[:].bitcast(I32))
+        move_rows(0, 1)
+        move_rows(0, 2)
         load_words(1, slice(T - TAIL, T))
         load_queries(0, 0)
         load_queries(0, 1)
-        make_plane(1)
+        move_rows(0, 3)
+        for i in range(1, 4):
+            move_rows(1, i)
 
         for t in range(Q_TILES):
             for o in range(PASSES):
@@ -150,13 +153,13 @@ def tile_picked_zlate_max_p_kernel(tc, x_words, x_scales, hT, offs, out):
         for piece in h_raw:
             interleave(*piece)
 
-        for step in range(4):
+        for step in range(6):
             nc.tensor.matmul_mx(
                 out=bank[Q_TILES - 1, 1][0:32, :],
-                lhsT=x_code[0, 0][:, 0:32].bitcast(FP8X4),
-                lhsT_scale=x_scale[0][:, 0:32],
-                rhs=x_code[0, 0][:].bitcast(FP8X4),
-                rhs_scale=x_scale[0][:, 0:N],
+                lhsT=x_code[0, N][:, 0:32].bitcast(FP8X4),
+                lhsT_scale=picked[:, N : N + 32],
+                rhs=x_code[0, N][:].bitcast(FP8X4),
+                rhs_scale=picked[:, N:S],
                 start=True,
                 stop=True,
             )
@@ -178,8 +181,12 @@ def tile_picked_zlate_max_p_kernel(tc, x_words, x_scales, hT, offs, out):
         pool_max(1, 0, h_raw[2, 0][:, 0])
         feed(2, 1)
         pool_max(1, 1, h_raw[2, 1][:, 0])
-        feed(3, 0)
-        feed(3, 1)
+        quantize(3, 0)
+        quantize(3, 1)
+        for first in (0, N):
+            multiply(3, 0, first)
+            multiply(3, 1, first)
+        multiply(3, 1, N + N // 2)
         for t in (2, 3):
             for h in range(HALVES):
                 pool_max(t, h, h_raw[3, 1][:, 2 * (t - 2) + h])

@@ -115,8 +115,8 @@ def tile_picked_zlate_max_p_kernel(tc, x_words, x_scales, hT, offs, out):
 
         columns_done = {key: 0 for key in bank}
 
-        def multiply(t, o, first):
-            count = x_code[o, first].shape[1]
+        def multiply(t, o, first, count):
+            start = max(f for which, f in x_code if which == o and f <= first)
             h, col = divmod(first, N)
             before = columns_done[t, h]
             columns_done[t, h] = before + count
@@ -124,7 +124,7 @@ def tile_picked_zlate_max_p_kernel(tc, x_words, x_scales, hT, offs, out):
                 out=bank[t, h][:, col : col + count],
                 lhsT=h_code[t, o][:].bitcast(FP8X4),
                 lhsT_scale=h_scale[t, o][:],
-                rhs=x_code[o, first][:].bitcast(FP8X4),
+                rhs=x_code[o, start][:, first - start : first - start + count].bitcast(FP8X4),
                 rhs_scale=x_scale[o][4 * o : P, first : first + count],
                 start=before == 0,
                 stop=before + count == PASSES * N,
@@ -133,7 +133,7 @@ def tile_picked_zlate_max_p_kernel(tc, x_words, x_scales, hT, offs, out):
         def feed(t, o, over=None):
             quantize(t, o, over)
             for first in sorted(f for which, f in x_code if which == o):
-                multiply(t, o, first)
+                multiply(t, o, first, x_code[o, first].shape[1])
 
         def tokens(t, h):
             return bank[t, h][:].rearrange("p (v d) -> p v d", d=D)
@@ -165,14 +165,15 @@ def tile_picked_zlate_max_p_kernel(tc, x_words, x_scales, hT, offs, out):
             )
         gather_words(1, 0, N)
         quantize(0, 0)
-        multiply(0, 0, 0)
-        multiply(0, 0, N)
+        multiply(0, 0, 0, N)
         gather_words(1, N, N // 2, "h_raw0_0")
         quantize(0, 1)
-        multiply(0, 1, 0)
-        multiply(0, 1, N)
+        multiply(0, 1, 0, N)
+        multiply(0, 1, N, N // 2)
+        multiply(0, 0, N, N // 2)
+        multiply(0, 0, N + N // 2, N // 2)
         gather_words(1, N + N // 2, N // 2, "h_raw0_1")
-        multiply(0, 1, N + N // 2)
+        multiply(0, 1, N + N // 2, N // 2)
         feed(1, 0)
         pool_max(0, 0, h_raw[1, 0][:, 0])
         feed(1, 1)
@@ -183,10 +184,11 @@ def tile_picked_zlate_max_p_kernel(tc, x_words, x_scales, hT, offs, out):
         pool_max(1, 1, h_raw[2, 1][:, 0])
         quantize(3, 0)
         quantize(3, 1)
-        for first in (0, N):
-            multiply(3, 0, first)
-            multiply(3, 1, first)
-        multiply(3, 1, N + N // 2)
+        multiply(3, 0, 0, N)
+        multiply(3, 1, 0, N)
+        multiply(3, 1, N, N // 2)
+        multiply(3, 1, N + N // 2, N // 2)
+        multiply(3, 0, N, N)
         for t in (2, 3):
             for h in range(HALVES):
                 pool_max(t, h, h_raw[3, 1][:, 2 * (t - 2) + h])

@@ -179,12 +179,12 @@ def tile_picked_zlate_max_p_kernel(tc, x_words, x_scales, hT, offs, out):
         feed(1, 1)
         pool_max(0, 1, h_raw[1, 1][:, 0])
         feed(2, 0)
-        pool_max(1, 0, h_raw[2, 0][:, 0])
         feed(2, 1)
-        pool_max(1, 1, h_raw[2, 1][:, 0])
+        pool_max(1, 0, h_raw[2, 1][:, 0])
         quantize(3, 0)
-        quantize(3, 1)
         multiply(3, 0, 0, N)
+        pool_max(1, 1, h_raw[3, 0][:, 0])
+        quantize(3, 1)
         multiply(3, 1, 0, N)
         multiply(3, 1, N, N // 2)
         multiply(3, 1, N + N // 2, N // 2)

from contextlib import ExitStack

import concourse.mybir as mybir

K, T, S, D, J = 1024, 4096, 1024, 4, 512
FLOPS = 2 * K * J * S

F32 = mybir.dt.float32
BF16 = mybir.dt.bfloat16
I32 = mybir.dt.int32
U32 = mybir.dt.uint32
U16 = mybir.dt.uint16
U8 = mybir.dt.uint8
FP8X4 = mybir.dt.float8_e4m3fn_x4
MAX = mybir.AluOpType.max

P = 128
PACK = 4
K_PASS = P * PACK
PASSES = K // K_PASS
N = 512
HALVES = S // N
Q_TILES = J // P
DOCS = N // D
ALIGN = 256
HEAD = 1024
TAIL = 1024


def tile_picked_zlate_max_p_kernel(tc, x_words, x_scales, hT, offs, out):
    nc = tc.nc
    with ExitStack() as ctx:
        keep = ctx.enter_context(tc.tile_pool(name="keep", bufs=1))
        psum = ctx.enter_context(tc.psum_pool(name="psum", bufs=1))

        def tile(shape, dtype, name, over=None):
            return keep.tile(shape, dtype, name=name, tag=over or name, align_bytes=ALIGN)

        scale_table = tile([P, T], U8, "scale_table")
        nc.vector.memset(scale_table[:].bitcast(I32), 0)

        word_table = [tile([P, T], I32, "word_table%d" % o) for o in range(PASSES)]
        offsets = keep.tile([P, S // 16], U16, name="offsets")
        picked = tile([P, S], U8, "picked")
        x_scale = [tile([P, S], U8, "x_scale%d" % o) for o in range(PASSES)]
        h_raw, h_bf, h_code, h_scale, x_code, bank = {}, {}, {}, {}, {}, {}

        def load_words(o, cols):
            words = x_words[o].rearrange("p n t -> p (n t)").bitcast(I32)
            nc.sync.dma_start(out=word_table[o][:, cols], in_=words[:, cols])

        def load_scales():
            nc.sync.dma_start(
                out=scale_table[0:P:4, :].bitcast(I32),
                in_=x_scales.rearrange("o m c -> m o c").bitcast(I32),
            )

        def load_queries(t, o):
            h_raw[t, o] = tile([P, PACK, P], F32, "h_raw%d_%d" % (t, o))
            rows = hT[o * K_PASS : (o + 1) * K_PASS, t * P : (t + 1) * P]
            nc.sync.dma_start(out=h_raw[t, o][:], in_=rows.rearrange("(p j) c -> p j c", j=PACK))

        def move_rows(o, i):
            nc.sync.dma_start(
                out=x_scale[o][4 * o + i : P : 32, :].bitcast(I32),
                in_=picked[4 * o + 8 * i : P : 32, :].bitcast(I32),
            )

        load_words(0, slice(0, HEAD))
        nc.sync.dma_start(offsets[:], offs)
        load_scales()
        load_words(0, slice(HEAD, T))
        load_words(1, slice(0, T - TAIL))
        nc.vector.tensor_copy(picked[:], scale_table[:].indirect(offsets[:]))
        for o in range(PASSES):
            nc.vector.tensor_copy(x_scale[o][:].bitcast(I32), picked[:].bitcast(I32))
        move_rows(0, 1)
        move_rows(0, 2)
        load_words(1, slice(T - TAIL, T))
        load_queries(0, 0)
        load_queries(0, 1)
        move_rows(0, 3)
        for i in range(1, 4):
            move_rows(1, i)

        for t in range(Q_TILES):
            for o in range(PASSES):
                if (t, o) not in h_raw:
                    load_queries(t, o)

        for t in range(Q_TILES):
            for h in range(HALVES):
                bank[t, h] = psum.tile([P, N], F32, name="bank%d_%d" % (t, h))

        def gather_words(o, first, count, over=None):
            x_code[o, first] = tile([P, count], U32, "x_code%d_%d" % (o, first), over)
            part = offsets[:, first // 16 : (first + count) // 16]
            nc.vector.tensor_copy(x_code[o, first][:], word_table[o][:].bitcast(U32).indirect(part))

        def interleave(t, o):
            h_bf[t, o] = tile([P, P, PACK], BF16, "h_bf%d_%d" % (t, o))
            nc.scalar.copy(
                out=h_bf[t, o][:].rearrange("p (c i) j -> p c j i", i=4),
                in_=h_raw[t, o][:].rearrange("p j (c i) -> p c j i", i=4),
            )

        def quantize(t, o, over=None):
            h_code[t, o] = tile([P, P], U32, "h_code%d_%d" % (t, o), over)
            h_scale[t, o] = tile([P, P], U8, "h_scale%d_%d" % (t, o))
            nc.vector.quantize_mx(
                out=h_code[t, o][:].bitcast(FP8X4),
                scales=h_scale[t, o][:],
                in_=h_bf[t, o][:].rearrange("p c j -> p (c j)"),
            )

        columns_done = {key: 0 for key in bank}

        def multiply(t, o, first, count):
            start = max(f for which, f in x_code if which == o and f <= first)
            h, col = divmod(first, N)
            before = columns_done[t, h]
            columns_done[t, h] = before + count
            nc.tensor.matmul_mx(
                out=bank[t, h][:, col : col + count],
                lhsT=h_code[t, o][:].bitcast(FP8X4),
                lhsT_scale=h_scale[t, o][:],
                rhs=x_code[o, start][:, first - start : first - start + count].bitcast(FP8X4),
                rhs_scale=x_scale[o][4 * o : P, first : first + count],
                start=before == 0,
                stop=before + count == PASSES * N,
            )

        def feed(t, o, over=None):
            quantize(t, o, over)
            for first in sorted(f for which, f in x_code if which == o):
                multiply(t, o, first, x_code[o, first].shape[1])

        def tokens(t, h):
            return bank[t, h][:].rearrange("p (v d) -> p v d", d=D)

        def bank_max(t, h, best):
            nc.vector.tensor_reduce(out=best, in_=tokens(t, h), axis=mybir.AxisListType.X, op=MAX)

        def store(t, docs, best):
            nc.sync.dma_start(out=out[t * P : (t + 1) * P, docs], in_=best)

        def pool_max(t, h, best):
            bank_max(t, h, best)
            store(t, slice(h * DOCS, (h + 1) * DOCS), best)

        for h in range(HALVES):
            gather_words(0, h * N, N)
        for piece in h_raw:
            interleave(*piece)

        for step in range(6):
            nc.tensor.matmul_mx(
                out=bank[Q_TILES - 1, 1][0:32, :],
                lhsT=x_code[0, N][:, 0:32].bitcast(FP8X4),
                lhsT_scale=picked[:, N : N + 32],
                rhs=x_code[0, N][:].bitcast(FP8X4),
                rhs_scale=picked[:, N:S],
                start=True,
                stop=True,
            )
        gather_words(1, 0, N)
        quantize(0, 0)
        multiply(0, 0, 0, N)
        gather_words(1, N, N // 2, "h_raw0_0")
        quantize(0, 1)
        multiply(0, 1, 0, N)
        multiply(0, 1, N, N // 2)
        multiply(0, 0, N, N // 2)
        multiply(0, 0, N + N // 2, N // 2)
        gather_words(1, N + N // 2, N // 2, "h_raw0_1")
        multiply(0, 1, N + N // 2, N // 2)
        feed(1, 0)
        pool_max(0, 0, h_raw[1, 0][:, 0])
        feed(1, 1)
        pool_max(0, 1, h_raw[1, 1][:, 0])
        feed(2, 0)
        feed(2, 1)
        pool_max(1, 0, h_raw[2, 1][:, 0])
        quantize(3, 0)
        multiply(3, 0, 0, N)
        pool_max(1, 1, h_raw[3, 0][:, 0])
        quantize(3, 1)
        multiply(3, 1, 0, N)
        multiply(3, 1, N, N // 2)
        multiply(3, 1, N + N // 2, N // 2)
        multiply(3, 0, N, N)
        for t in (2, 3):
            for h in range(HALVES):
                pool_max(t, h, h_raw[3, 1][:, 2 * (t - 2) + h])
